import numpy as np
import ml_dtypes


def mxq(x, axis, fmt="e4m3"):
    dtype, down = {"e4m3": (ml_dtypes.float8_e4m3fn, 7), "e5m2": (ml_dtypes.float8_e5m2, 14)}[fmt]
    v = np.moveaxis(np.asarray(x, np.float32).astype(ml_dtypes.bfloat16).astype(np.float64), axis, -1)
    blocks = v.reshape(v.shape[:-1] + (-1, 32))
    amax = np.abs(blocks).max(-1, keepdims=True)
    byte = np.maximum(np.where(amax > 0, np.frexp(amax)[1] - 1 + 127, 0) - down, 1)
    scale = np.exp2(byte - 127.0)
    codes = (blocks / scale).astype(np.float32).astype(dtype).astype(np.float64)
    return np.moveaxis((codes * scale).reshape(v.shape), -1, axis)


WIDE = False


def mx_kscale(k):
    if not WIDE:
        return np.ones(k)
    levels = np.array([10, -10, 5, -5, 0])
    if k % 512:
        return np.exp2(np.random.permutation(np.resize(levels, k // 32))).repeat(32)
    a = np.empty((k // 512, 16))
    for p in range(k // 512):
        a[p, :8] = np.random.permutation(np.resize(levels, 8))
        for g in range(8):
            far = levels[np.abs(levels - a[p, g]) >= 10]
            a[p, g + 8] = far[np.random.randint(len(far))]
    return np.exp2(a.ravel()).repeat(32)


def f64(x):
    return np.asarray(x).astype(np.float64)


def striped(idx):
    return np.tile(idx.reshape(-1, 16).T, (8, 1)).astype(np.uint16)


def unstriped(offs):
    return offs[:16].T.reshape(-1).astype(np.int64)


def pack_weight(w):
    k, n = w.shape
    w = f64(np.asarray(w, np.float32).astype(ml_dtypes.bfloat16)).reshape(k // 32, 32, n)
    amax = np.abs(w).max(1)
    byte = np.clip(np.where(amax > 0, np.frexp(amax)[1] - 1 + 127 - 7, 1), 1, 254)
    scaled = (w * np.exp2(127.0 - byte)[:, None, :]).reshape(k, n).astype(np.float32)
    words = np.ascontiguousarray(scaled.reshape(k // 512, 128, 4, n).transpose(0, 1, 3, 2)).astype(ml_dtypes.float8_e4m3fn).view(np.uint8)
    return words, np.ascontiguousarray(byte.astype(np.uint8).reshape(k // 512, 16, n))


def unpack_weight(words, scales):
    g, p, n, _ = words.shape
    vals = np.ascontiguousarray(words).view(ml_dtypes.float8_e4m3fn).astype(np.float64) * np.repeat(np.exp2(scales.astype(np.float64) - 127.0), 8, axis=1)[..., None]
    return vals.transpose(0, 1, 3, 2).reshape(g * 512, n)


K, T, S, D, V, H, N = 512, 1024, 512, 4, 256, 512, 256
P = 2 ** 7


def setup_inputs():
    n = np.random.standard_normal
    s = mx_kscale(K)[:, None]
    u = mx_kscale(H)
    packed_w2 = pack_weight(n((H, N)) / np.sqrt(H) / u[:, None])
    return {
        "xT": (n((K, T)) * s).astype(np.float32),
        "w1": (n((K, H)) / np.sqrt(K) / s * u).astype(np.float32),
        "w2_words": packed_w2[0],
        "w2_scales": packed_w2[1],
        "gate": (np.tile(np.random.uniform(0.2, 1.0, (D, 1, V)) / np.sqrt(D), (1, P, 1))).astype(np.float32),
        "offs": striped(np.random.permutation(T)[:S]),
        "cen": striped(np.random.permutation(S)[:V]),
        "pos1": striped(np.random.permutation(S)[:V]),
        "pos2": striped(np.random.permutation(S)[:V]),
        "pos3": striped(np.random.permutation(S)[:V]),
        "pos4": striped(np.random.permutation(S)[:V]),
    }


def reference(xT, w1, w2_words, w2_scales, gate, offs, cen, pos1, pos2, pos3, pos4):
    xq = mxq(f64(xT)[:, unstriped(offs)], 0, "e4m3")
    h = mxq(f64(w1), 0, "e4m3").T @ xq
    z = h[:, unstriped(cen)] - (h[:, unstriped(pos1)] * f64(gate)[0, :1] + h[:, unstriped(pos2)] * f64(gate)[1, :1] + h[:, unstriped(pos3)] * f64(gate)[2, :1] + h[:, unstriped(pos4)] * f64(gate)[3, :1])
    return unpack_weight(w2_words, w2_scales).T @ mxq(z, 0, "e4m3")

@@ -1,0 +1,205 @@
+from contextlib import ExitStack
+
+import concourse.mybir as mybir
+from concourse.masks import make_identity
+
+K, T, S, D, V, H, N = 512, 1024, 512, 4, 256, 512, 256
+FLOPS = 2 * K * H * S + 2 * H * N * V
+
+F32 = mybir.dt.float32
+BF16 = mybir.dt.bfloat16
+I32 = mybir.dt.int32
+U32 = mybir.dt.uint32
+U16 = mybir.dt.uint16
+U8 = mybir.dt.uint8
+FP8X4 = mybir.dt.float8_e4m3fn_x4
+COPY = mybir.ActivationFunctionType.Copy
+MULT = mybir.AluOpType.mult
+
+P = 128
+PACK = 4
+TILES = H // P
+SH = S // 2
+LANES = 16
+
+
+def tile_picked_lapl_none_e_kernel(
+    tc, xT, w1, w2_words, w2_scales, gate, offs, cen, pos1, pos2, pos3, pos4, out
+):
+    nc = tc.nc
+    with ExitStack() as ctx:
+        keep = ctx.enter_context(tc.tile_pool(name="keep", bufs=1))
+        psum = ctx.enter_context(tc.psum_pool(name="psum", bufs=1))
+
+        def sb(name, shape, dtype, tag=None):
+            return keep.tile(shape, dtype, name=name, tag=tag or name, align_bytes=64)
+
+        def bank(number, name, shape):
+            return psum.tile(shape, F32, name=name, tag="bank%d" % number)
+
+        ident = sb("ident", [P, P], F32)
+        make_identity(nc, ident[:])
+        offs_sb = sb("offs_sb", [P, S // LANES], U16)
+        gate_rows = sb("gate_rows", [P, V], F32)
+        nc.vector.memset(gate_rows[:], 0.0)
+        nc.sync.dma_start(offs_sb[:], offs)
+        x_rows = xT.rearrange("(p j) t -> j p t", j=PACK)
+        planes = []
+        for j in range(PACK):
+            plane = sb("plane%d" % j, [P, T], F32)
+            nc.sync.dma_start(plane[:], x_rows[j])
+            planes.append(plane)
+            if j == 1:
+                nc.sync.dma_start(gate_rows[0:D, :], gate[:, 0, :])
+        w1_rows = w1.rearrange("(p j) c -> p j c", j=PACK)
+        w1_first = sb("w1_first", [P, PACK, P], F32)
+        nc.sync.dma_start(w1_first[:], w1_rows[:, :, 0:P])
+        lists = []
+        for name, source in (("pos1", pos1), ("pos2", pos2), ("pos3", pos3), ("pos4", pos4), ("cen", cen)):
+            held = sb(name + "_sb", [P, V // LANES], U16)
+            nc.sync.dma_start(held[:], source)
+            lists.append(held)
+        w1_rest = sb("w1_rest", [P, PACK, H - P], F32)
+        nc.sync.dma_start(w1_rest[:], w1_rows[:, :, P:H])
+        w2_codes = sb("w2_codes", [P, N], U32)
+        nc.sync.dma_start(w2_codes[:].bitcast(I32), w2_words[0].rearrange("p n t -> p (n t)").bitcast(I32))
+        w2_plane = sb("w2_plane", [P, N], U8)
+        nc.gpsimd.memset(w2_plane[:], 0)
+        for q in range(4):
+            nc.sync.dma_start(
+                w2_plane[32 * q : 32 * q + 4, :].bitcast(I32), w2_scales[0, 4 * q : 4 * q + 4, :].bitcast(I32)
+            )
+
+        turned = bank(4, "turned", [P, 2, P])
+        for half in range(2):
+            nc.tensor.transpose(turned[:, half, :], gate_rows[:, half * P : (half + 1) * P], ident[:])
+        gate_cols = sb("gate_cols", [P, 2, D], F32)
+        nc.scalar.activation(gate_cols[:], turned[:, :, 0:D], COPY, scale=-1.0)
+        minus_gate = []
+        for pair in range(2):
+            spread = bank(pair, "spread%d" % pair, [P, 2, 2, P])
+            for dd in range(2):
+                d = 2 * pair + dd
+                for half in range(2):
+                    nc.tensor.transpose(
+                        spread[:, dd, half, :], gate_cols[:, half, d : d + 1].to_broadcast([P, P]), ident[:]
+                    )
+            weights = sb("minus_gate%d" % pair, [P, 2, V], F32)
+            nc.scalar.copy(weights[:].rearrange("p d v -> p (d v)"), spread[:].rearrange("p d h c -> p (d h c)"))
+            minus_gate += [weights[:, 0, :], weights[:, 1, :]]
+
+        x_grouped = [sb("x_grouped%d" % s, [P, SH, PACK], BF16) for s in range(2)]
+        low = sb("low", [P, 2, S], BF16)
+        for j in range(2):
+            nc.vector.tensor_copy(low[:, j, :], planes[j][:].indirect(offs_sb[:]))
+        for s in range(2):
+            nc.scalar.copy(x_grouped[s][:, :, 0:2], low[:, :, s * SH : (s + 1) * SH].rearrange("p j c -> p c j"))
+        high = [sb("high%d" % s, [P, 2, SH], BF16) for s in range(2)]
+        for j in range(2):
+            for s in range(2):
+                piece = offs_sb[:, s * SH // LANES : (s + 1) * SH // LANES]
+                nc.vector.tensor_copy(high[s][:, j, :], planes[2 + j][:].indirect(piece))
+        for s in range(2):
+            nc.vector.tensor_copy(x_grouped[s][:, :, 2:4], high[s][:].rearrange("p j c -> p c j"))
+
+        w1_codes, w1_planes = [], []
+
+        def quantize_w1(t):
+            raw = w1_first[:] if t == 0 else w1_rest[:, :, (t - 1) * P : t * P]
+            grouped = sb("w1_grouped%d" % t, [P, P, PACK], BF16)
+            nc.scalar.copy(
+                grouped[:].rearrange("p (c i) j -> p c j i", i=4), raw.rearrange("p j (c i) -> p c j i", i=4)
+            )
+            codes = sb("w1_codes%d" % t, [P, P], U32)
+            plane = sb("w1_plane%d" % t, [P, P], U8)
+            nc.vector.quantize_mx(codes[:].bitcast(FP8X4), plane[:], grouped[:].rearrange("p c j -> p (c j)"))
+            w1_codes.append(codes)
+            w1_planes.append(plane)
+
+        quantize_w1(0)
+        x_codes = sb("x_codes", [P, S], U32)
+        x_plane = sb("x_plane", [P, S], U8)
+        for s in range(2):
+            cols = slice(s * SH, (s + 1) * SH)
+            nc.vector.quantize_mx(
+                x_codes[:, cols].bitcast(FP8X4), x_plane[:, cols], x_grouped[s][:].rearrange("p c j -> p (c j)")
+            )
+
+        def first_product(t, number, cols, h_tile):
+            acc = bank(number, "acc%d_%d" % (t, cols.start), [P, cols.stop - cols.start])
+            nc.tensor.matmul_mx(
+                acc[:], w1_codes[t][:].bitcast(FP8X4), w1_planes[t][:], x_codes[:, cols].bitcast(FP8X4),
+                x_plane[:, cols], start=True, stop=True,
+            )
+            nc.scalar.copy(h_tile[:, cols], acc[:])
+
+        h = [sb("h%d" % t, [P, S], F32) for t in range(TILES)]
+        for s in range(2):
+            first_product(0, 2 + s, slice(s * SH, (s + 1) * SH), h[0])
+
+        z_turned = [sb("z_turned%d" % half, [P, 2, P, 2], BF16) for half in range(2)]
+
+        def gather(t, u, half):
+            cols = slice(0, V) if half is None else slice(half * P, (half + 1) * P)
+            entries = lists[u][:, cols.start // LANES : cols.stop // LANES]
+            tag = "w1_grouped%d" % (t + 1) if u == 2 and t + 1 < TILES else None
+            term = sb("term%d_%d_%d" % (t, u, cols.start), [P, cols.stop - cols.start], F32, tag)
+            if u < D:
+                nc.vector.tensor_tensor(term[:], h[t][:].indirect(entries), minus_gate[u][:, cols], MULT)
+            else:
+                nc.vector.tensor_copy(term[:], h[t][:].indirect(entries))
+            return term
+
+        def add_turned(acc, term, u):
+            nc.tensor.matmul(acc[:], term, ident[:], start=(u == 0), stop=(u == D), is_transpose=True)
+
+        def round_out(t, half, acc):
+            nc.scalar.copy(
+                z_turned[half][:, :, 32 * t : 32 * (t + 1), :], acc[:].rearrange("p (q u e) -> p u q e", u=2, e=2)
+            )
+
+        def second_product(half):
+            back = bank(4 + half, "back%d" % half, [P, 2, P])
+            words = z_turned[half][:].rearrange("p u q e -> p (u q e)").bitcast(F32)
+            for u in range(2):
+                nc.tensor.transpose(back[:, u, :], words[:, u * P : (u + 1) * P], ident[:])
+            z_grouped = sb("z_grouped%d" % half, [P, P * PACK], BF16)
+            nc.scalar.copy(
+                z_grouped[:].bitcast(F32).rearrange("p (v u) -> p v u", u=2), back[:].rearrange("p u v -> p v u")
+            )
+            z_codes = sb("z_codes%d" % half, [P, P], U32)
+            z_plane = sb("z_plane%d" % half, [P, P], U8)
+            nc.vector.quantize_mx(z_codes[:].bitcast(FP8X4), z_plane[:], z_grouped[:])
+            acc = bank(2 + half, "result%d" % half, [P, 2, P])
+            for m in range(2):
+                cols = slice(m * P, (m + 1) * P)
+                nc.tensor.matmul_mx(
+                    acc[:, m, :], w2_codes[:, cols].bitcast(FP8X4), w2_plane[:, cols], z_codes[:].bitcast(FP8X4),
+                    z_plane[:], start=True, stop=True,
+                )
+            result = sb("result_sb%d" % half, [P, 2, P], F32)
+            nc.scalar.copy(result[:], acc[:])
+            nc.sync.dma_start(
+                out.rearrange("(m p) v -> p m v", p=P)[:, :, half * P : (half + 1) * P], result[:]
+            )
+
+        h_banks = {1: 4, 2: 5, 3: 2}
+        for t in range(TILES):
+            if t + 1 < TILES:
+                quantize_w1(t + 1)
+                first_product(t + 1, h_banks[t + 1], slice(0, S), h[t + 1])
+            sums = [bank(6 * (t % 2) + half, "sum%d_%d" % (t, half), [P, P]) for half in range(2)]
+            if t + 1 < TILES:
+                for u in range(D + 1):
+                    term = gather(t, u, None)
+                    for half in range(2):
+                        add_turned(sums[half], term[:, half * P : (half + 1) * P], u)
+                for half in range(2):
+                    round_out(t, half, sums[half])
+            else:
+                for half in range(2):
+                    for u in range(D + 1):
+                        add_turned(sums[half], gather(t, u, half)[:], u)
+                    round_out(t, half, sums[half])
+                for half in range(2):
+                    second_product(half)

@@ -15,12 +15,13 @@ U8 = mybir.dt.uint8
 FP8X4 = mybir.dt.float8_e4m3fn_x4
 COPY = mybir.ActivationFunctionType.Copy
 MULT = mybir.AluOpType.mult
+ADD = mybir.AluOpType.add
 
 P = 128
 PACK = 4
-TILES = H // P
 SH = S // 2
 LANES = 16
+CEN = D
 
 
 def tile_picked_lapl_none_e_kernel(
@@ -37,34 +38,34 @@ def tile_picked_lapl_none_e_kernel(
         def bank(number, name, shape):
             return psum.tile(shape, F32, name=name, tag="bank%d" % number)
 
+        gate_rows = sb("gate_rows", [P, V], F32)
+        nc.gpsimd.memset(gate_rows[:], 0.0)
         ident = sb("ident", [P, P], F32)
         make_identity(nc, ident[:])
-        offs_sb = sb("offs_sb", [P, S // LANES], U16)
-        gate_rows = sb("gate_rows", [P, V], F32)
-        nc.vector.memset(gate_rows[:], 0.0)
-        nc.sync.dma_start(offs_sb[:], offs)
-        x_rows = xT.rearrange("(p j) t -> j p t", j=PACK)
-        planes = []
-        for j in range(PACK):
-            plane = sb("plane%d" % j, [P, T], F32)
-            nc.sync.dma_start(plane[:], x_rows[j])
-            planes.append(plane)
-            if j == 1:
-                nc.sync.dma_start(gate_rows[0:D, :], gate[:, 0, :])
-        w1_rows = w1.rearrange("(p j) c -> p j c", j=PACK)
-        w1_first = sb("w1_first", [P, PACK, P], F32)
-        nc.sync.dma_start(w1_first[:], w1_rows[:, :, 0:P])
-        lists = []
-        for name, source in (("pos1", pos1), ("pos2", pos2), ("pos3", pos3), ("pos4", pos4), ("cen", cen)):
-            held = sb(name + "_sb", [P, V // LANES], U16)
-            nc.sync.dma_start(held[:], source)
-            lists.append(held)
-        w1_rest = sb("w1_rest", [P, PACK, H - P], F32)
-        nc.sync.dma_start(w1_rest[:], w1_rows[:, :, P:H])
-        w2_codes = sb("w2_codes", [P, N], U32)
-        nc.sync.dma_start(w2_codes[:].bitcast(I32), w2_words[0].rearrange("p n t -> p (n t)").bitcast(I32))
         w2_plane = sb("w2_plane", [P, N], U8)
         nc.gpsimd.memset(w2_plane[:], 0)
+
+        x_rows = xT.rearrange("(p j) t -> j p t", j=PACK)
+        planes = [sb("plane%d" % j, [P, T], F32) for j in range(PACK)]
+        offs_sb = sb("offs_sb", [P, S // LANES], U16)
+        nc.sync.dma_start(planes[0][:], x_rows[0])
+        nc.sync.dma_start(offs_sb[:], offs)
+        nc.sync.dma_start(gate_rows[0:D, :], gate[:, 0, :])
+        for j in range(1, PACK):
+            nc.sync.dma_start(planes[j][:], x_rows[j])
+        w1_rows = w1.rearrange("(p j) c -> p j c", j=PACK)
+        w1_raw = []
+        for side in range(2):
+            raw = sb("w1_raw%d" % side, [P, PACK, H // 2], F32)
+            for rows in ((slice(0, 2), slice(2, 4)) if side == 0 else (slice(0, 4),)):
+                nc.sync.dma_start(raw[:, rows, :], w1_rows[:, rows, side * H // 2 : (side + 1) * H // 2])
+            w1_raw.append(raw[:].rearrange("p j (m f) -> p m j f", f=PACK))
+        lists = {}
+        for u, name, source in ((CEN, "cen", cen), (0, "pos1", pos1), (1, "pos2", pos2), (2, "pos3", pos3), (3, "pos4", pos4)):
+            lists[u] = sb(name + "_sb", [P, V // LANES], U16)
+            nc.sync.dma_start(lists[u][:], source)
+        w2_codes = sb("w2_codes", [P, N], U32)
+        nc.sync.dma_start(w2_codes[:].bitcast(I32), w2_words[0].rearrange("p n t -> p (n t)").bitcast(I32))
         for q in range(4):
             nc.sync.dma_start(
                 w2_plane[32 * q : 32 * q + 4, :].bitcast(I32), w2_scales[0, 4 * q : 4 * q + 4, :].bitcast(I32)
@@ -94,112 +95,148 @@ def tile_picked_lapl_none_e_kernel(
             nc.vector.tensor_copy(low[:, j, :], planes[j][:].indirect(offs_sb[:]))
         for s in range(2):
             nc.scalar.copy(x_grouped[s][:, :, 0:2], low[:, :, s * SH : (s + 1) * SH].rearrange("p j c -> p c j"))
-        high = [sb("high%d" % s, [P, 2, SH], BF16) for s in range(2)]
-        for j in range(2):
-            for s in range(2):
-                piece = offs_sb[:, s * SH // LANES : (s + 1) * SH // LANES]
-                nc.vector.tensor_copy(high[s][:, j, :], planes[2 + j][:].indirect(piece))
+        high = sb("high", [P, 2, S], BF16)
+        nc.vector.tensor_copy(high[:, 0, :], planes[2][:].indirect(offs_sb[:]))
         for s in range(2):
-            nc.vector.tensor_copy(x_grouped[s][:, :, 2:4], high[s][:].rearrange("p j c -> p c j"))
+            piece = offs_sb[:, s * SH // LANES : (s + 1) * SH // LANES]
+            nc.vector.tensor_copy(high[:, 1, s * SH : (s + 1) * SH], planes[3][:].indirect(piece))
+        for s in range(2):
+            nc.vector.tensor_copy(x_grouped[s][:, :, 2:4], high[:, :, s * SH : (s + 1) * SH].rearrange("p j c -> p c j"))
 
-        w1_codes, w1_planes = [], []
+        w1_mx = {}
 
-        def quantize_w1(t):
-            raw = w1_first[:] if t == 0 else w1_rest[:, :, (t - 1) * P : t * P]
-            grouped = sb("w1_grouped%d" % t, [P, P, PACK], BF16)
-            nc.scalar.copy(
-                grouped[:].rearrange("p (c i) j -> p c j i", i=4), raw.rearrange("p j (c i) -> p c j i", i=4)
-            )
-            codes = sb("w1_codes%d" % t, [P, P], U32)
-            plane = sb("w1_plane%d" % t, [P, P], U8)
+        def quantize_paired(side):
+            grouped = sb("w1_paired%d" % side, [P, P, PACK], BF16)
+            dealt = grouped[:].rearrange("p (m e) j -> p m j e", e=2)
+            for rows in ((slice(0, 2), slice(2, 4)) if side == 0 else (slice(0, 4),)):
+                nc.scalar.copy(dealt[:, :, rows, :], w1_raw[side][:, :, rows, 0:2])
+            codes = sb("w1_codes%d" % side, [P, P], U32)
+            plane = sb("w1_plane%d" % side, [P, P], U8)
             nc.vector.quantize_mx(codes[:].bitcast(FP8X4), plane[:], grouped[:].rearrange("p c j -> p (c j)"))
-            w1_codes.append(codes)
-            w1_planes.append(plane)
+            w1_mx[side] = (codes[:], plane[:])
 
-        quantize_w1(0)
+        def quantize_single():
+            grouped = sb("w1_single", [P, 2, P, PACK], BF16)
+            for side in range(2):
+                nc.scalar.copy(
+                    grouped[:, :, 64 * side : 64 * (side + 1), :].rearrange("p s m j -> p m j s"),
+                    w1_raw[side][:, :, :, 2:4],
+                )
+            codes = sb("w1_codes_single", [P, 2 * P], U32)
+            plane = sb("w1_plane_single", [P, 2 * P], U8)
+            nc.vector.quantize_mx(codes[:].bitcast(FP8X4), plane[:], grouped[:].rearrange("p s c j -> p (s c j)"))
+            for slot in range(2):
+                w1_mx[2 + slot] = (codes[:, slot * P : (slot + 1) * P], plane[:, slot * P : (slot + 1) * P])
+
+        quantize_paired(0)
         x_codes = sb("x_codes", [P, S], U32)
-        x_plane = sb("x_plane", [P, S], U8)
+        x_plane = sb("x_plane", [P, S], U8, "w1_paired0")
         for s in range(2):
             cols = slice(s * SH, (s + 1) * SH)
             nc.vector.quantize_mx(
                 x_codes[:, cols].bitcast(FP8X4), x_plane[:, cols], x_grouped[s][:].rearrange("p c j -> p (c j)")
             )
 
-        def first_product(t, number, cols, h_tile):
+        h = [sb("h%d" % t, [P, S], F32) for t in range(PACK)]
+
+        def first_product(t, number, cols, on_vector=False):
             acc = bank(number, "acc%d_%d" % (t, cols.start), [P, cols.stop - cols.start])
+            codes, plane = w1_mx[t]
             nc.tensor.matmul_mx(
-                acc[:], w1_codes[t][:].bitcast(FP8X4), w1_planes[t][:], x_codes[:, cols].bitcast(FP8X4),
-                x_plane[:, cols], start=True, stop=True,
+                acc[:], codes.bitcast(FP8X4), plane, x_codes[:, cols].bitcast(FP8X4), x_plane[:, cols],
+                start=True, stop=True,
             )
-            nc.scalar.copy(h_tile[:, cols], acc[:])
-
-        h = [sb("h%d" % t, [P, S], F32) for t in range(TILES)]
-        for s in range(2):
-            first_product(0, 2 + s, slice(s * SH, (s + 1) * SH), h[0])
-
-        z_turned = [sb("z_turned%d" % half, [P, 2, P, 2], BF16) for half in range(2)]
-
-        def gather(t, u, half):
-            cols = slice(0, V) if half is None else slice(half * P, (half + 1) * P)
-            entries = lists[u][:, cols.start // LANES : cols.stop // LANES]
-            tag = "w1_grouped%d" % (t + 1) if u == 2 and t + 1 < TILES else None
-            term = sb("term%d_%d_%d" % (t, u, cols.start), [P, cols.stop - cols.start], F32, tag)
-            if u < D:
-                nc.vector.tensor_tensor(term[:], h[t][:].indirect(entries), minus_gate[u][:, cols], MULT)
+            if on_vector:
+                nc.vector.tensor_copy(h[t][:, cols], acc[:])
             else:
-                nc.vector.tensor_copy(term[:], h[t][:].indirect(entries))
-            return term
+                nc.scalar.copy(h[t][:, cols], acc[:])
 
-        def add_turned(acc, term, u):
-            nc.tensor.matmul(acc[:], term, ident[:], start=(u == 0), stop=(u == D), is_transpose=True)
+        def summed_terms(t, order, first_bank, held):
+            sums = [bank(first_bank + half, "sum%d_%d" % (t, half), [P, P]) for half in range(2)]
+            for n, u in enumerate(order):
+                term = sb("term%d_%d" % (t, u), [P, V], F32, held if n == (0 if t == 0 else 2) else None)
+                if u == CEN:
+                    nc.vector.tensor_copy(term[:], h[t][:].indirect(lists[u][:]))
+                else:
+                    nc.vector.tensor_tensor(term[:], h[t][:].indirect(lists[u][:]), minus_gate[u], MULT)
+                for half in range(2):
+                    nc.tensor.matmul(
+                        sums[half][:], term[:, half * P : (half + 1) * P], ident[:],
+                        start=(n == 0), stop=(n == len(order) - 1), is_transpose=True,
+                    )
+            return sums
 
-        def round_out(t, half, acc):
-            nc.scalar.copy(
-                z_turned[half][:, :, 32 * t : 32 * (t + 1), :], acc[:].rearrange("p (q u e) -> p u q e", u=2, e=2)
+        z_pairs = [sb("z_pairs%d" % half, [P, P, 2], BF16) for half in range(2)]
+
+        def paired_tile(side, first_bank, held):
+            sums = summed_terms(side, [CEN, 0, 1, 2, 3], first_bank, held)
+            for half in range(2):
+                nc.scalar.copy(
+                    z_pairs[half][:, 64 * side : 64 * (side + 1), :].rearrange("p m e -> p (m e)"), sums[half][:]
+                )
+
+        def single_tile(slot, first_bank, held, pulls):
+            sums = summed_terms(2 + slot, [0, 1, 2, 3], first_bank, held)
+            for half in range(2):
+                staged = sb("staged%d_%d" % (slot, half), [P, P], F32)
+                nc.scalar.copy(staged[:], sums[half][:])
+                nc.tensor.transpose(pulls[half][:, slot, :], staged[:], ident[:])
+
+        first_product(0, 2, slice(0, SH))
+        first_product(0, 3, slice(SH, SH + P))
+        first_product(0, 4, slice(SH + P, S), True)
+        quantize_single()
+        first_product(2, 4, slice(0, S))
+        first_product(3, 5, slice(0, S))
+        paired_tile(0, 6, "w1_single")
+        quantize_paired(1)
+        first_product(1, 2, slice(0, S))
+        pulls = [bank(3 + half, "pulls%d" % half, [P, 2, P]) for half in range(2)]
+        single_tile(0, 0, None, pulls)
+        single_tile(1, 6, "w1_paired1", pulls)
+        paired_tile(1, 0, None)
+
+        own = sb("own", [P, 2, 2, P], F32, "h1")
+        z_grouped = [sb("z_grouped%d" % half, [P, P, PACK], BF16) for half in range(2)]
+        for half in range(2):
+            back = bank((5, 2)[half], "back%d" % half, [P, P])
+            nc.tensor.transpose(back[:], z_pairs[half][:].rearrange("p m e -> p (m e)").bitcast(F32), ident[:])
+            words = z_grouped[half][:].rearrange("p v j -> p (v j)").bitcast(F32).rearrange("p (v u) -> p v u", u=2)
+            nc.scalar.copy(words[:, :, 0], back[:])
+        for half in range(2):
+            entries = lists[CEN][:, half * P // LANES : (half + 1) * P // LANES]
+            for slot in range(2):
+                nc.vector.tensor_copy(own[:, half, slot, :], h[2 + slot][:].indirect(entries))
+        for half in range(2):
+            nc.vector.tensor_tensor(
+                z_grouped[half][:, :, 2:4], pulls[half][:].rearrange("p s v -> p v s"),
+                own[:, half, :, :].rearrange("p s v -> p v s"), ADD,
             )
-
-        def second_product(half):
-            back = bank(4 + half, "back%d" % half, [P, 2, P])
-            words = z_turned[half][:].rearrange("p u q e -> p (u q e)").bitcast(F32)
-            for u in range(2):
-                nc.tensor.transpose(back[:, u, :], words[:, u * P : (u + 1) * P], ident[:])
-            z_grouped = sb("z_grouped%d" % half, [P, P * PACK], BF16)
-            nc.scalar.copy(
-                z_grouped[:].bitcast(F32).rearrange("p (v u) -> p v u", u=2), back[:].rearrange("p u v -> p v u")
-            )
+        out_rows = out.rearrange("(m p) v -> p m v", p=P)
+        for half in range(2):
             z_codes = sb("z_codes%d" % half, [P, P], U32)
             z_plane = sb("z_plane%d" % half, [P, P], U8)
-            nc.vector.quantize_mx(z_codes[:].bitcast(FP8X4), z_plane[:], z_grouped[:])
-            acc = bank(2 + half, "result%d" % half, [P, 2, P])
+            nc.vector.quantize_mx(
+                z_codes[:].bitcast(FP8X4), z_plane[:], z_grouped[half][:].rearrange("p v j -> p (v j)")
+            )
+            accs = [bank((6, 6, 7, 0)[2 * half + m], "result%d_%d" % (half, m), [P, P]) for m in range(2)] if half else None
+            both = None if half else bank(6, "result0", [P, 2, P])
             for m in range(2):
                 cols = slice(m * P, (m + 1) * P)
                 nc.tensor.matmul_mx(
-                    acc[:, m, :], w2_codes[:, cols].bitcast(FP8X4), w2_plane[:, cols], z_codes[:].bitcast(FP8X4),
-                    z_plane[:], start=True, stop=True,
+                    accs[m][:] if half else both[:, m, :], w2_codes[:, cols].bitcast(FP8X4), w2_plane[:, cols],
+                    z_codes[:].bitcast(FP8X4), z_plane[:], start=True, stop=True,
                 )
-            result = sb("result_sb%d" % half, [P, 2, P], F32)
-            nc.scalar.copy(result[:], acc[:])
-            nc.sync.dma_start(
-                out.rearrange("(m p) v -> p m v", p=P)[:, :, half * P : (half + 1) * P], result[:]
-            )
-
-        h_banks = {1: 4, 2: 5, 3: 2}
-        for t in range(TILES):
-            if t + 1 < TILES:
-                quantize_w1(t + 1)
-                first_product(t + 1, h_banks[t + 1], slice(0, S), h[t + 1])
-            sums = [bank(6 * (t % 2) + half, "sum%d_%d" % (t, half), [P, P]) for half in range(2)]
-            if t + 1 < TILES:
-                for u in range(D + 1):
-                    term = gather(t, u, None)
-                    for half in range(2):
-                        add_turned(sums[half], term[:, half * P : (half + 1) * P], u)
-                for half in range(2):
-                    round_out(t, half, sums[half])
+            if half == 0:
+                result = sb("result_sb0", [P, 2, P], F32)
+                nc.scalar.copy(result[:], both[:])
+                nc.sync.dma_start(out_rows[:, :, 0:P], result[:])
             else:
-                for half in range(2):
-                    for u in range(D + 1):
-                        add_turned(sums[half], gather(t, u, half)[:], u)
-                    round_out(t, half, sums[half])
-                for half in range(2):
-                    second_product(half)
+                for m in range(2):
+                    last = sb("last%d" % m, [P, P], F32)
+                    if m == 0:
+                        nc.scalar.copy(last[:], accs[m][:])
+                        nc.scalar.dma_start(out_rows[:, m, P:V], last[:])
+                    else:
+                        nc.vector.tensor_copy(last[:], accs[m][:])
+                        nc.sync.dma_start(out_rows[:, m, P:V], last[:])

@@ -15,7 +15,7 @@ U8 = mybir.dt.uint8
 FP8X4 = mybir.dt.float8_e4m3fn_x4
 COPY = mybir.ActivationFunctionType.Copy
 MULT = mybir.AluOpType.mult
-ADD = mybir.AluOpType.add
+SUBTRACT = mybir.AluOpType.subtract
 
 P = 128
 PACK = 4
@@ -38,10 +38,10 @@ def tile_picked_lapl_none_e_kernel(
         def bank(number, name, shape):
             return psum.tile(shape, F32, name=name, tag="bank%d" % number)
 
-        gate_rows = sb("gate_rows", [P, V], F32)
-        nc.gpsimd.memset(gate_rows[:], 0.0)
         ident = sb("ident", [P, P], F32)
         make_identity(nc, ident[:])
+        minus_one = sb("minus_one", [P, V], F32)
+        nc.gpsimd.memset(minus_one[:], -1.0)
         w2_plane = sb("w2_plane", [P, N], U8)
         nc.gpsimd.memset(w2_plane[:], 0)
 
@@ -50,7 +50,6 @@ def tile_picked_lapl_none_e_kernel(
         offs_sb = sb("offs_sb", [P, S // LANES], U16)
         nc.sync.dma_start(planes[0][:], x_rows[0])
         nc.sync.dma_start(offs_sb[:], offs)
-        nc.sync.dma_start(gate_rows[0:D, :], gate[:, 0, :])
         for j in range(1, PACK):
             nc.sync.dma_start(planes[j][:], x_rows[j])
         w1_rows = w1.rearrange("(p j) c -> p j c", j=PACK)
@@ -60,34 +59,20 @@ def tile_picked_lapl_none_e_kernel(
             for rows in ((slice(0, 2), slice(2, 4)) if side == 0 else (slice(0, 4),)):
                 nc.sync.dma_start(raw[:, rows, :], w1_rows[:, rows, side * H // 2 : (side + 1) * H // 2])
             w1_raw.append(raw[:].rearrange("p j (m f) -> p m j f", f=PACK))
-        lists = {}
+        lists, factors = {}, {CEN: minus_one[:]}
         for u, name, source in ((CEN, "cen", cen), (0, "pos1", pos1), (1, "pos2", pos2), (2, "pos3", pos3), (3, "pos4", pos4)):
             lists[u] = sb(name + "_sb", [P, V // LANES], U16)
             nc.sync.dma_start(lists[u][:], source)
+            if u in (0, 2):
+                weights = sb("gate%d" % u, [P, 2, V], F32)
+                nc.sync.dma_start(weights[:], gate[u : u + 2].rearrange("d p v -> p d v"))
+                factors[u], factors[u + 1] = weights[:, 0, :], weights[:, 1, :]
         w2_codes = sb("w2_codes", [P, N], U32)
         nc.sync.dma_start(w2_codes[:].bitcast(I32), w2_words[0].rearrange("p n t -> p (n t)").bitcast(I32))
         for q in range(4):
             nc.sync.dma_start(
                 w2_plane[32 * q : 32 * q + 4, :].bitcast(I32), w2_scales[0, 4 * q : 4 * q + 4, :].bitcast(I32)
             )
-
-        turned = bank(4, "turned", [P, 2, P])
-        for half in range(2):
-            nc.tensor.transpose(turned[:, half, :], gate_rows[:, half * P : (half + 1) * P], ident[:])
-        gate_cols = sb("gate_cols", [P, 2, D], F32)
-        nc.scalar.activation(gate_cols[:], turned[:, :, 0:D], COPY, scale=-1.0)
-        minus_gate = []
-        for pair in range(2):
-            spread = bank(pair, "spread%d" % pair, [P, 2, 2, P])
-            for dd in range(2):
-                d = 2 * pair + dd
-                for half in range(2):
-                    nc.tensor.transpose(
-                        spread[:, dd, half, :], gate_cols[:, half, d : d + 1].to_broadcast([P, P]), ident[:]
-                    )
-            weights = sb("minus_gate%d" % pair, [P, 2, V], F32)
-            nc.scalar.copy(weights[:].rearrange("p d v -> p (d v)"), spread[:].rearrange("p d h c -> p (d h c)"))
-            minus_gate += [weights[:, 0, :], weights[:, 1, :]]
 
         x_grouped = [sb("x_grouped%d" % s, [P, SH, PACK], BF16) for s in range(2)]
         low = sb("low", [P, 2, S], BF16)
@@ -106,7 +91,7 @@ def tile_picked_lapl_none_e_kernel(
         w1_mx = {}
 
         def quantize_paired(side):
-            grouped = sb("w1_paired%d" % side, [P, P, PACK], BF16)
+            grouped = sb("w1_paired%d" % side, [P, P, PACK], BF16, (None, "w1_plane0")[side])
             dealt = grouped[:].rearrange("p (m e) j -> p m j e", e=2)
             for rows in ((slice(0, 2), slice(2, 4)) if side == 0 else (slice(0, 4),)):
                 nc.scalar.copy(dealt[:, :, rows, :], w1_raw[side][:, :, rows, 0:2])
@@ -116,7 +101,7 @@ def tile_picked_lapl_none_e_kernel(
             w1_mx[side] = (codes[:], plane[:])
 
         def quantize_single():
-            grouped = sb("w1_single", [P, 2, P, PACK], BF16)
+            grouped = sb("w1_single", [P, 2, P, PACK], BF16, "w1_codes0")
             for side in range(2):
                 nc.scalar.copy(
                     grouped[:, :, 64 * side : 64 * (side + 1), :].rearrange("p s m j -> p m j s"),
@@ -129,36 +114,31 @@ def tile_picked_lapl_none_e_kernel(
                 w1_mx[2 + slot] = (codes[:, slot * P : (slot + 1) * P], plane[:, slot * P : (slot + 1) * P])
 
         quantize_paired(0)
-        x_codes = sb("x_codes", [P, S], U32)
-        x_plane = sb("x_plane", [P, S], U8, "w1_paired0")
+        x_mx = []
         for s in range(2):
-            cols = slice(s * SH, (s + 1) * SH)
-            nc.vector.quantize_mx(
-                x_codes[:, cols].bitcast(FP8X4), x_plane[:, cols], x_grouped[s][:].rearrange("p c j -> p (c j)")
-            )
+            codes = sb("x_codes%d" % s, [P, SH], U32)
+            plane = sb("x_plane%d" % s, [P, SH], U8, "w1_paired0" if s == 1 else None)
+            nc.vector.quantize_mx(codes[:].bitcast(FP8X4), plane[:], x_grouped[s][:].rearrange("p c j -> p (c j)"))
+            x_mx.append((codes[:], plane[:]))
 
         h = [sb("h%d" % t, [P, S], F32) for t in range(PACK)]
 
-        def first_product(t, number, cols, on_vector=False):
-            acc = bank(number, "acc%d_%d" % (t, cols.start), [P, cols.stop - cols.start])
+        def first_product(t, number, sides, engine_copy):
+            acc = bank(number, "acc%d_%d" % (t, sides[0]), [P, len(sides), SH])
             codes, plane = w1_mx[t]
-            nc.tensor.matmul_mx(
-                acc[:], codes.bitcast(FP8X4), plane, x_codes[:, cols].bitcast(FP8X4), x_plane[:, cols],
-                start=True, stop=True,
-            )
-            if on_vector:
-                nc.vector.tensor_copy(h[t][:, cols], acc[:])
-            else:
-                nc.scalar.copy(h[t][:, cols], acc[:])
+            for n, s in enumerate(sides):
+                nc.tensor.matmul_mx(
+                    acc[:, n, :], codes.bitcast(FP8X4), plane, x_mx[s][0].bitcast(FP8X4), x_mx[s][1],
+                    start=True, stop=True,
+                )
+            engine_copy(h[t][:, sides[0] * SH : (sides[-1] + 1) * SH], acc[:].rearrange("p n c -> p (n c)"))
 
         def summed_terms(t, order, first_bank, held):
             sums = [bank(first_bank + half, "sum%d_%d" % (t, half), [P, P]) for half in range(2)]
+            late = sb("late%d" % t, [P, len(order) - 2, V], F32, held)
             for n, u in enumerate(order):
-                term = sb("term%d_%d" % (t, u), [P, V], F32, held if n == (0 if t == 0 else 2) else None)
-                if u == CEN:
-                    nc.vector.tensor_copy(term[:], h[t][:].indirect(lists[u][:]))
-                else:
-                    nc.vector.tensor_tensor(term[:], h[t][:].indirect(lists[u][:]), minus_gate[u], MULT)
+                term = sb("term%d_%d" % (t, u), [P, V], F32)[:] if n < 2 else late[:, n - 2, :]
+                nc.vector.tensor_tensor(term, h[t][:].indirect(lists[u][:]), factors[u], MULT)
                 for half in range(2):
                     nc.tensor.matmul(
                         sums[half][:], term[:, half * P : (half + 1) * P], ident[:],
@@ -171,46 +151,52 @@ def tile_picked_lapl_none_e_kernel(
         def paired_tile(side, first_bank, held):
             sums = summed_terms(side, [CEN, 0, 1, 2, 3], first_bank, held)
             for half in range(2):
-                nc.scalar.copy(
-                    z_pairs[half][:, 64 * side : 64 * (side + 1), :].rearrange("p m e -> p (m e)"), sums[half][:]
+                nc.scalar.activation(
+                    z_pairs[half][:, 64 * side : 64 * (side + 1), :].rearrange("p m e -> p (m e)"), sums[half][:],
+                    COPY, scale=-1.0,
                 )
 
         def single_tile(slot, first_bank, held, pulls):
-            sums = summed_terms(2 + slot, [0, 1, 2, 3], first_bank, held)
+            sums = summed_terms(2 + slot, [0, 1, 2], first_bank, held)
             for half in range(2):
                 staged = sb("staged%d_%d" % (slot, half), [P, P], F32)
                 nc.scalar.copy(staged[:], sums[half][:])
                 nc.tensor.transpose(pulls[half][:, slot, :], staged[:], ident[:])
 
-        first_product(0, 2, slice(0, SH))
-        first_product(0, 3, slice(SH, SH + P))
-        first_product(0, 4, slice(SH + P, S), True)
-        quantize_single()
-        first_product(2, 4, slice(0, S))
-        first_product(3, 5, slice(0, S))
-        paired_tile(0, 6, "w1_single")
+        first_product(0, 2, [0], nc.scalar.copy)
+        first_product(0, 3, [1], nc.vector.tensor_copy)
         quantize_paired(1)
-        first_product(1, 2, slice(0, S))
-        pulls = [bank(3 + half, "pulls%d" % half, [P, 2, P]) for half in range(2)]
-        single_tile(0, 0, None, pulls)
-        single_tile(1, 6, "w1_paired1", pulls)
-        paired_tile(1, 0, None)
-
-        own = sb("own", [P, 2, 2, P], F32, "h1")
+        first_product(1, 2, [0, 1], nc.scalar.copy)
+        paired_tile(0, 6, "w1_plane0")
+        quantize_single()
+        first_product(2, 3, [0, 1], nc.scalar.copy)
+        first_product(3, 5, [0, 1], nc.scalar.copy)
+        paired_tile(1, 0, "w1_codes0")
         z_grouped = [sb("z_grouped%d" % half, [P, P, PACK], BF16) for half in range(2)]
         for half in range(2):
-            back = bank((5, 2)[half], "back%d" % half, [P, P])
+            back = bank((2, 4)[half], "back%d" % half, [P, P])
             nc.tensor.transpose(back[:], z_pairs[half][:].rearrange("p m e -> p (m e)").bitcast(F32), ident[:])
             words = z_grouped[half][:].rearrange("p v j -> p (v j)").bitcast(F32).rearrange("p (v u) -> p v u", u=2)
             nc.scalar.copy(words[:, :, 0], back[:])
+        pulls = [bank((3, 5)[half], "pulls%d" % half, [P, 2, P]) for half in range(2)]
+        single_tile(0, 6, None, pulls)
+        single_tile(1, 0, None, pulls)
+
+        kept = sb("kept", [P, 2, V], F32)
+        for slot in range(2):
+            nc.vector.tensor_tensor(kept[:, slot, :], h[2 + slot][:].indirect(lists[D - 1][:]), factors[D - 1], MULT)
+        own = sb("own", [P, 2, 2, P], F32, "term3_1")
         for half in range(2):
             entries = lists[CEN][:, half * P // LANES : (half + 1) * P // LANES]
             for slot in range(2):
-                nc.vector.tensor_copy(own[:, half, slot, :], h[2 + slot][:].indirect(entries))
+                nc.vector.tensor_tensor(
+                    own[:, half, slot, :], h[2 + slot][:].indirect(entries), kept[:, slot, half * P : (half + 1) * P],
+                    SUBTRACT,
+                )
         for half in range(2):
             nc.vector.tensor_tensor(
-                z_grouped[half][:, :, 2:4], pulls[half][:].rearrange("p s v -> p v s"),
-                own[:, half, :, :].rearrange("p s v -> p v s"), ADD,
+                z_grouped[half][:, :, 2:4], own[:, half, :, :].rearrange("p s v -> p v s"),
+                pulls[half][:].rearrange("p s v -> p v s"), SUBTRACT,
             )
         out_rows = out.rearrange("(m p) v -> p m v", p=P)
         for half in range(2):
@@ -219,7 +205,7 @@ def tile_picked_lapl_none_e_kernel(
             nc.vector.quantize_mx(
                 z_codes[:].bitcast(FP8X4), z_plane[:], z_grouped[half][:].rearrange("p v j -> p (v j)")
             )
-            accs = [bank((6, 6, 7, 0)[2 * half + m], "result%d_%d" % (half, m), [P, P]) for m in range(2)] if half else None
+            accs = [bank((6, 6, 7, 2)[2 * half + m], "result%d_%d" % (half, m), [P, P]) for m in range(2)] if half else None
             both = None if half else bank(6, "result0", [P, 2, P])
             for m in range(2):
                 cols = slice(m * P, (m + 1) * P)

@@ -91,7 +91,7 @@ def tile_picked_lapl_none_e_kernel(
         w1_mx = {}
 
         def quantize_paired(side):
-            grouped = sb("w1_paired%d" % side, [P, P, PACK], BF16, (None, "w1_plane0")[side])
+            grouped = sb("w1_paired%d" % side, [P, P, PACK], BF16)
             dealt = grouped[:].rearrange("p (m e) j -> p m j e", e=2)
             for rows in ((slice(0, 2), slice(2, 4)) if side == 0 else (slice(0, 4),)):
                 nc.scalar.copy(dealt[:, :, rows, :], w1_raw[side][:, :, rows, 0:2])
@@ -119,19 +119,22 @@ def tile_picked_lapl_none_e_kernel(
             codes = sb("x_codes%d" % s, [P, SH], U32)
             plane = sb("x_plane%d" % s, [P, SH], U8, "w1_paired0" if s == 1 else None)
             nc.vector.quantize_mx(codes[:].bitcast(FP8X4), plane[:], x_grouped[s][:].rearrange("p c j -> p (c j)"))
-            x_mx.append((codes[:], plane[:]))
+            x_mx.append((codes, plane))
 
         h = [sb("h%d" % t, [P, S], F32) for t in range(PACK)]
 
-        def first_product(t, number, sides, engine_copy):
-            acc = bank(number, "acc%d_%d" % (t, sides[0]), [P, len(sides), SH])
+        def first_product(t, number, start, stop, engine_copy):
+            acc = bank(number, "acc%d_%d" % (t, start), [P, stop - start])
             codes, plane = w1_mx[t]
-            for n, s in enumerate(sides):
+            for first in range(start, stop, SH):
+                width = min(SH, stop - first)
+                cols = slice(first % SH, first % SH + width)
+                x_codes, x_plane = x_mx[first // SH]
                 nc.tensor.matmul_mx(
-                    acc[:, n, :], codes.bitcast(FP8X4), plane, x_mx[s][0].bitcast(FP8X4), x_mx[s][1],
-                    start=True, stop=True,
+                    acc[:, first - start : first - start + width], codes.bitcast(FP8X4), plane,
+                    x_codes[:, cols].bitcast(FP8X4), x_plane[:, cols], start=True, stop=True,
                 )
-            engine_copy(h[t][:, sides[0] * SH : (sides[-1] + 1) * SH], acc[:].rearrange("p n c -> p (n c)"))
+            engine_copy(h[t][:, start:stop], acc[:])
 
         def summed_terms(t, order, first_bank, held):
             sums = [bank(first_bank + half, "sum%d_%d" % (t, half), [P, P]) for half in range(2)]
@@ -163,14 +166,15 @@ def tile_picked_lapl_none_e_kernel(
                 nc.scalar.copy(staged[:], sums[half][:])
                 nc.tensor.transpose(pulls[half][:, slot, :], staged[:], ident[:])
 
-        first_product(0, 2, [0], nc.scalar.copy)
-        first_product(0, 3, [1], nc.vector.tensor_copy)
+        first_product(0, 2, 0, SH, nc.scalar.copy)
+        first_product(0, 3, SH, SH + P, nc.scalar.copy)
+        first_product(0, 4, SH + P, S, nc.vector.tensor_copy)
         quantize_paired(1)
-        first_product(1, 2, [0, 1], nc.scalar.copy)
-        paired_tile(0, 6, "w1_plane0")
+        first_product(1, 2, 0, S, nc.scalar.copy)
+        paired_tile(0, 6, "w1_paired1")
         quantize_single()
-        first_product(2, 3, [0, 1], nc.scalar.copy)
-        first_product(3, 5, [0, 1], nc.scalar.copy)
+        first_product(2, 3, 0, S, nc.scalar.copy)
+        first_product(3, 5, 0, S, nc.scalar.copy)
         paired_tile(1, 0, "w1_codes0")
         z_grouped = [sb("z_grouped%d" % half, [P, P, PACK], BF16) for half in range(2)]
         for half in range(2):
@@ -186,20 +190,23 @@ def tile_picked_lapl_none_e_kernel(
         for slot in range(2):
             nc.vector.tensor_tensor(kept[:, slot, :], h[2 + slot][:].indirect(lists[D - 1][:]), factors[D - 1], MULT)
         own = sb("own", [P, 2, 2, P], F32, "term3_1")
-        for half in range(2):
+
+        def own_term(half, slot):
             entries = lists[CEN][:, half * P // LANES : (half + 1) * P // LANES]
-            for slot in range(2):
-                nc.vector.tensor_tensor(
-                    own[:, half, slot, :], h[2 + slot][:].indirect(entries), kept[:, slot, half * P : (half + 1) * P],
-                    SUBTRACT,
-                )
-        for half in range(2):
+            nc.vector.tensor_tensor(
+                own[:, half, slot, :], h[2 + slot][:].indirect(entries), kept[:, slot, half * P : (half + 1) * P],
+                SUBTRACT,
+            )
+
+        def finish_z(half):
             nc.vector.tensor_tensor(
                 z_grouped[half][:, :, 2:4], own[:, half, :, :].rearrange("p s v -> p v s"),
                 pulls[half][:].rearrange("p s v -> p v s"), SUBTRACT,
             )
+
         out_rows = out.rearrange("(m p) v -> p m v", p=P)
-        for half in range(2):
+
+        def second_product(half):
             z_codes = sb("z_codes%d" % half, [P, P], U32)
             z_plane = sb("z_plane%d" % half, [P, P], U8)
             nc.vector.quantize_mx(
@@ -226,3 +233,12 @@ def tile_picked_lapl_none_e_kernel(
                     else:
                         nc.vector.tensor_copy(last[:], accs[m][:])
                         nc.sync.dma_start(out_rows[:, m, P:V], last[:])
+
+        own_term(0, 0)
+        own_term(0, 1)
+        own_term(1, 0)
+        finish_z(0)
+        own_term(1, 1)
+        second_product(0)
+        finish_z(1)
+        second_product(1)

@@ -22,6 +22,9 @@ PACK = 4
 SH = S // 2
 LANES = 16
 CEN = D
+SIDE = P // 2
+PIECES = ((0, SH), (SH, SH + P), (SH + P, S))
+EARLY = 3
 
 
 def tile_picked_lapl_none_e_kernel(
@@ -41,141 +44,148 @@ def tile_picked_lapl_none_e_kernel(
         ident = sb("ident", [P, P], F32)
         make_identity(nc, ident[:])
         minus_one = sb("minus_one", [P, V], F32)
-        nc.gpsimd.memset(minus_one[:], -1.0)
+        nc.vector.memset(minus_one[:], -1.0)
         w2_plane = sb("w2_plane", [P, N], U8)
         nc.gpsimd.memset(w2_plane[:], 0)
 
         x_rows = xT.rearrange("(p j) t -> j p t", j=PACK)
-        planes = [sb("plane%d" % j, [P, T], F32) for j in range(PACK)]
+        x_slots = [sb("x_slot%d" % j, [P, T], F32) for j in range(PACK)]
         offs_sb = sb("offs_sb", [P, S // LANES], U16)
-        nc.sync.dma_start(planes[0][:], x_rows[0])
+        nc.sync.dma_start(x_slots[0][:], x_rows[0])
         nc.sync.dma_start(offs_sb[:], offs)
         for j in range(1, PACK):
-            nc.sync.dma_start(planes[j][:], x_rows[j])
+            nc.sync.dma_start(x_slots[j][:], x_rows[j])
         w1_rows = w1.rearrange("(p j) c -> p j c", j=PACK)
         w1_raw = []
         for side in range(2):
             raw = sb("w1_raw%d" % side, [P, PACK, H // 2], F32)
-            for rows in ((slice(0, 2), slice(2, 4)) if side == 0 else (slice(0, 4),)):
-                nc.sync.dma_start(raw[:, rows, :], w1_rows[:, rows, side * H // 2 : (side + 1) * H // 2])
+            nc.sync.dma_start(raw[:], w1_rows[:, :, side * H // 2 : (side + 1) * H // 2])
             w1_raw.append(raw[:].rearrange("p j (m f) -> p m j f", f=PACK))
         lists, factors = {}, {CEN: minus_one[:]}
         for u, name, source in ((CEN, "cen", cen), (0, "pos1", pos1), (1, "pos2", pos2), (2, "pos3", pos3), (3, "pos4", pos4)):
             lists[u] = sb(name + "_sb", [P, V // LANES], U16)
             nc.sync.dma_start(lists[u][:], source)
-            if u in (0, 2):
-                weights = sb("gate%d" % u, [P, 2, V], F32)
-                nc.sync.dma_start(weights[:], gate[u : u + 2].rearrange("d p v -> p d v"))
-                factors[u], factors[u + 1] = weights[:, 0, :], weights[:, 1, :]
+        gate_sb = sb("gate_sb", [P, D, V], F32)
+        nc.sync.dma_start(gate_sb[:], gate.rearrange("d p v -> p d v"))
+        for u in range(D):
+            factors[u] = gate_sb[:, u, :]
         w2_codes = sb("w2_codes", [P, N], U32)
         nc.sync.dma_start(w2_codes[:].bitcast(I32), w2_words[0].rearrange("p n t -> p (n t)").bitcast(I32))
-        for q in range(4):
+        for r in range(4):
             nc.sync.dma_start(
-                w2_plane[32 * q : 32 * q + 4, :].bitcast(I32), w2_scales[0, 4 * q : 4 * q + 4, :].bitcast(I32)
+                w2_plane[32 * r : 32 * r + 4, :].bitcast(I32), w2_scales[0, 4 * r : 4 * r + 4, :].bitcast(I32)
             )
 
-        x_grouped = [sb("x_grouped%d" % s, [P, SH, PACK], BF16) for s in range(2)]
+        halves = [slice(half * SH, (half + 1) * SH) for half in range(2)]
+        x_grouped = [sb("x_grouped%d" % half, [P, SH, PACK], BF16) for half in range(2)]
         low = sb("low", [P, 2, S], BF16)
         for j in range(2):
-            nc.vector.tensor_copy(low[:, j, :], planes[j][:].indirect(offs_sb[:]))
-        for s in range(2):
-            nc.scalar.copy(x_grouped[s][:, :, 0:2], low[:, :, s * SH : (s + 1) * SH].rearrange("p j c -> p c j"))
+            nc.vector.tensor_copy(low[:, j, :], x_slots[j][:].indirect(offs_sb[:]))
+        for grouped, nodes in zip(x_grouped, halves):
+            nc.scalar.copy(grouped[:, :, 0:2], low[:, :, nodes].rearrange("p j c -> p c j"))
         high = sb("high", [P, 2, S], BF16)
-        nc.vector.tensor_copy(high[:, 0, :], planes[2][:].indirect(offs_sb[:]))
-        for s in range(2):
-            piece = offs_sb[:, s * SH // LANES : (s + 1) * SH // LANES]
-            nc.vector.tensor_copy(high[:, 1, s * SH : (s + 1) * SH], planes[3][:].indirect(piece))
-        for s in range(2):
-            nc.vector.tensor_copy(x_grouped[s][:, :, 2:4], high[:, :, s * SH : (s + 1) * SH].rearrange("p j c -> p c j"))
+        nc.vector.tensor_copy(high[:, 0, :], x_slots[2][:].indirect(offs_sb[:]))
+        for nodes in halves:
+            entries = offs_sb[:, nodes.start // LANES : nodes.stop // LANES]
+            nc.vector.tensor_copy(high[:, 1, nodes], x_slots[3][:].indirect(entries))
+        for grouped, nodes in zip(x_grouped, halves):
+            nc.vector.tensor_copy(grouped[:, :, 2:4], high[:, :, nodes].rearrange("p j c -> p c j"))
 
-        w1_mx = {}
+        w1_mx, w1_paired = {}, {}
+
+        def deal_paired(side, engine_copy, tag):
+            w1_paired[side] = sb("w1_paired%d" % side, [P, P, PACK], BF16, tag)
+            engine_copy(w1_paired[side][:].rearrange("p (m e) j -> p m j e", e=2), w1_raw[side][:, :, :, 0:2])
 
         def quantize_paired(side):
-            grouped = sb("w1_paired%d" % side, [P, P, PACK], BF16)
-            dealt = grouped[:].rearrange("p (m e) j -> p m j e", e=2)
-            for rows in ((slice(0, 2), slice(2, 4)) if side == 0 else (slice(0, 4),)):
-                nc.scalar.copy(dealt[:, :, rows, :], w1_raw[side][:, :, rows, 0:2])
             codes = sb("w1_codes%d" % side, [P, P], U32)
             plane = sb("w1_plane%d" % side, [P, P], U8)
-            nc.vector.quantize_mx(codes[:].bitcast(FP8X4), plane[:], grouped[:].rearrange("p c j -> p (c j)"))
+            nc.vector.quantize_mx(codes[:].bitcast(FP8X4), plane[:], w1_paired[side][:].rearrange("p c j -> p (c j)"))
             w1_mx[side] = (codes[:], plane[:])
 
+        w1_single = sb("w1_single", [P, 2, P, PACK], BF16)
+
+        def deal_single(side, start, stop, engine_copy):
+            engine_copy(
+                w1_single[:, :, SIDE * side + start : SIDE * side + stop, :].rearrange("p s m j -> p m j s"),
+                w1_raw[side][:, start:stop, :, 2:4],
+            )
+
         def quantize_single():
-            grouped = sb("w1_single", [P, 2, P, PACK], BF16, "w1_codes0")
-            for side in range(2):
-                nc.scalar.copy(
-                    grouped[:, :, 64 * side : 64 * (side + 1), :].rearrange("p s m j -> p m j s"),
-                    w1_raw[side][:, :, :, 2:4],
-                )
             codes = sb("w1_codes_single", [P, 2 * P], U32)
             plane = sb("w1_plane_single", [P, 2 * P], U8)
-            nc.vector.quantize_mx(codes[:].bitcast(FP8X4), plane[:], grouped[:].rearrange("p s c j -> p (s c j)"))
-            for slot in range(2):
-                w1_mx[2 + slot] = (codes[:, slot * P : (slot + 1) * P], plane[:, slot * P : (slot + 1) * P])
+            nc.vector.quantize_mx(codes[:].bitcast(FP8X4), plane[:], w1_single[:].rearrange("p s c j -> p (s c j)"))
+            for s in range(2):
+                w1_mx[2 + s] = (codes[:, s * P : (s + 1) * P], plane[:, s * P : (s + 1) * P])
 
+        deal_paired(0, nc.scalar.copy, None)
         quantize_paired(0)
+        deal_single(0, 0, SIDE, nc.scalar.copy)
+        x_codes = [sb("x_codes0", [P, SH], U32), sb("x_codes1", [P, SH], U32, "w1_paired0")]
+        x_planes = [sb("x_plane%d" % half, [P, SH], U8) for half in range(2)]
         x_mx = []
-        for s in range(2):
-            codes = sb("x_codes%d" % s, [P, SH], U32)
-            plane = sb("x_plane%d" % s, [P, SH], U8, "w1_paired0" if s == 1 else None)
-            nc.vector.quantize_mx(codes[:].bitcast(FP8X4), plane[:], x_grouped[s][:].rearrange("p c j -> p (c j)"))
+        for start, stop in PIECES:
+            half, cols = start // SH, slice(start % SH, start % SH + stop - start)
+            codes, plane = x_codes[half][:, cols], x_planes[half][:, cols]
+            nc.vector.quantize_mx(codes.bitcast(FP8X4), plane, x_grouped[half][:, cols, :].rearrange("p c j -> p (c j)"))
             x_mx.append((codes, plane))
 
         h = [sb("h%d" % t, [P, S], F32) for t in range(PACK)]
 
-        def first_product(t, number, start, stop, engine_copy):
+        def first_product(t, number, start, stop):
             acc = bank(number, "acc%d_%d" % (t, start), [P, stop - start])
             codes, plane = w1_mx[t]
-            for first in range(start, stop, SH):
-                width = min(SH, stop - first)
-                cols = slice(first % SH, first % SH + width)
-                x_codes, x_plane = x_mx[first // SH]
-                nc.tensor.matmul_mx(
-                    acc[:, first - start : first - start + width], codes.bitcast(FP8X4), plane,
-                    x_codes[:, cols].bitcast(FP8X4), x_plane[:, cols], start=True, stop=True,
-                )
-            engine_copy(h[t][:, start:stop], acc[:])
+            for (first, last), (piece_codes, piece_plane) in zip(PIECES, x_mx):
+                if start <= first and last <= stop:
+                    nc.tensor.matmul_mx(
+                        acc[:, first - start : last - start], codes.bitcast(FP8X4), plane,
+                        piece_codes.bitcast(FP8X4), piece_plane, start=True, stop=True,
+                    )
+            nc.scalar.copy(h[t][:, start:stop], acc[:])
 
-        def summed_terms(t, order, first_bank, held):
+        def summed_terms(t, order, first_bank, terms):
             sums = [bank(first_bank + half, "sum%d_%d" % (t, half), [P, P]) for half in range(2)]
-            late = sb("late%d" % t, [P, len(order) - 2, V], F32, held)
             for n, u in enumerate(order):
-                term = sb("term%d_%d" % (t, u), [P, V], F32)[:] if n < 2 else late[:, n - 2, :]
-                nc.vector.tensor_tensor(term, h[t][:].indirect(lists[u][:]), factors[u], MULT)
+                nc.vector.tensor_tensor(terms[n], h[t][:].indirect(lists[u][:]), factors[u], MULT)
                 for half in range(2):
                     nc.tensor.matmul(
-                        sums[half][:], term[:, half * P : (half + 1) * P], ident[:],
+                        sums[half][:], terms[n][:, half * P : (half + 1) * P], ident[:],
                         start=(n == 0), stop=(n == len(order) - 1), is_transpose=True,
                     )
             return sums
 
         z_pairs = [sb("z_pairs%d" % half, [P, P, 2], BF16) for half in range(2)]
 
-        def paired_tile(side, first_bank, held):
-            sums = summed_terms(side, [CEN, 0, 1, 2, 3], first_bank, held)
+        def paired_tile(side, first_bank, terms):
+            sums = summed_terms(side, [CEN] + list(range(D)), first_bank, terms)
             for half in range(2):
                 nc.scalar.activation(
-                    z_pairs[half][:, 64 * side : 64 * (side + 1), :].rearrange("p m e -> p (m e)"), sums[half][:],
+                    z_pairs[half][:, SIDE * side : SIDE * (side + 1), :].rearrange("p m e -> p (m e)"), sums[half][:],
                     COPY, scale=-1.0,
                 )
 
-        def single_tile(slot, first_bank, held, pulls):
-            sums = summed_terms(2 + slot, [0, 1, 2], first_bank, held)
+        def single_tile(s, first_bank, terms, pulls):
+            sums = summed_terms(2 + s, list(range(D - 1)), first_bank, terms)
             for half in range(2):
-                staged = sb("staged%d_%d" % (slot, half), [P, P], F32)
+                staged = sb("staged%d_%d" % (s, half), [P, P], F32)
                 nc.scalar.copy(staged[:], sums[half][:])
-                nc.tensor.transpose(pulls[half][:, slot, :], staged[:], ident[:])
+                nc.tensor.transpose(pulls[half][:, s, :], staged[:], ident[:])
 
-        first_product(0, 2, 0, SH, nc.scalar.copy)
-        first_product(0, 3, SH, SH + P, nc.scalar.copy)
-        first_product(0, 4, SH + P, S, nc.vector.tensor_copy)
-        quantize_paired(1)
-        first_product(1, 2, 0, S, nc.scalar.copy)
-        paired_tile(0, 6, "w1_paired1")
+        deal_single(1, 0, SIDE // 2, nc.vector.tensor_copy)
+        deal_single(1, SIDE // 2, SIDE, nc.scalar.copy)
+        deal_paired(1, nc.vector.tensor_copy, "x_grouped1")
+        for number, (start, stop) in enumerate(PIECES):
+            first_product(0, 2 + number, start, stop)
         quantize_single()
-        first_product(2, 3, 0, S, nc.scalar.copy)
-        first_product(3, 5, 0, S, nc.scalar.copy)
-        paired_tile(1, 0, "w1_codes0")
+        quantize_paired(1)
+        terms_early = sb("terms_early", [P, EARLY, V], F32)
+        terms_late = sb("terms_late", [P, D + 1 - EARLY, V], F32)
+        first_product(1, 5, 0, S)
+        paired_tile(0, 6, [terms_early[:, n, :] for n in range(EARLY)] + [terms_late[:, n, :] for n in range(D + 1 - EARLY)])
+        first_product(2, 3, 0, S)
+        first_product(3, 2, 0, S)
+        terms_second = sb("terms_second", [P, D + 1, V], F32, "terms_early")
+        paired_tile(1, 0, [terms_second[:, n, :] for n in range(D + 1)])
         z_grouped = [sb("z_grouped%d" % half, [P, P, PACK], BF16) for half in range(2)]
         for half in range(2):
             back = bank((2, 4)[half], "back%d" % half, [P, P])
@@ -183,24 +193,24 @@ def tile_picked_lapl_none_e_kernel(
             words = z_grouped[half][:].rearrange("p v j -> p (v j)").bitcast(F32).rearrange("p (v u) -> p v u", u=2)
             nc.scalar.copy(words[:, :, 0], back[:])
         pulls = [bank((3, 5)[half], "pulls%d" % half, [P, 2, P]) for half in range(2)]
-        single_tile(0, 6, None, pulls)
-        single_tile(1, 0, None, pulls)
+        terms_single = sb("terms_single", [P, 2, D, V], F32, "terms_late")
+        single_tile(0, 6, [terms_single[:, 0, n, :] for n in range(D - 1)], pulls)
+        single_tile(1, 0, [terms_single[:, 1, n, :] for n in range(D - 1)], pulls)
 
-        kept = sb("kept", [P, 2, V], F32)
-        for slot in range(2):
-            nc.vector.tensor_tensor(kept[:, slot, :], h[2 + slot][:].indirect(lists[D - 1][:]), factors[D - 1], MULT)
-        own = sb("own", [P, 2, 2, P], F32, "term3_1")
+        kept = terms_single[:, :, D - 1, :]
+        for s in range(2):
+            nc.vector.tensor_tensor(kept[:, s, :], h[2 + s][:].indirect(lists[D - 1][:]), factors[D - 1], MULT)
+        own = sb("own", [P, 2, V], F32)
 
-        def own_term(half, slot):
-            entries = lists[CEN][:, half * P // LANES : (half + 1) * P // LANES]
+        def own_term(s, start, stop):
+            entries = lists[CEN][:, start // LANES : stop // LANES]
             nc.vector.tensor_tensor(
-                own[:, half, slot, :], h[2 + slot][:].indirect(entries), kept[:, slot, half * P : (half + 1) * P],
-                SUBTRACT,
+                own[:, s, start:stop], h[2 + s][:].indirect(entries), kept[:, s, start:stop], SUBTRACT
             )
 
         def finish_z(half):
             nc.vector.tensor_tensor(
-                z_grouped[half][:, :, 2:4], own[:, half, :, :].rearrange("p s v -> p v s"),
+                z_grouped[half][:, :, 2:4], own[:, :, half * P : (half + 1) * P].rearrange("p s v -> p v s"),
                 pulls[half][:].rearrange("p s v -> p v s"), SUBTRACT,
             )
 
@@ -212,33 +222,22 @@ def tile_picked_lapl_none_e_kernel(
             nc.vector.quantize_mx(
                 z_codes[:].bitcast(FP8X4), z_plane[:], z_grouped[half][:].rearrange("p v j -> p (v j)")
             )
-            accs = [bank((6, 6, 7, 2)[2 * half + m], "result%d_%d" % (half, m), [P, P]) for m in range(2)] if half else None
-            both = None if half else bank(6, "result0", [P, 2, P])
             for m in range(2):
+                acc = bank((6, 7, 2, 4)[2 * half + m], "result%d_%d" % (half, m), [P, P])
                 cols = slice(m * P, (m + 1) * P)
                 nc.tensor.matmul_mx(
-                    accs[m][:] if half else both[:, m, :], w2_codes[:, cols].bitcast(FP8X4), w2_plane[:, cols],
+                    acc[:], w2_codes[:, cols].bitcast(FP8X4), w2_plane[:, cols],
                     z_codes[:].bitcast(FP8X4), z_plane[:], start=True, stop=True,
                 )
-            if half == 0:
-                result = sb("result_sb0", [P, 2, P], F32)
-                nc.scalar.copy(result[:], both[:])
-                nc.sync.dma_start(out_rows[:, :, 0:P], result[:])
-            else:
-                for m in range(2):
-                    last = sb("last%d" % m, [P, P], F32)
-                    if m == 0:
-                        nc.scalar.copy(last[:], accs[m][:])
-                        nc.scalar.dma_start(out_rows[:, m, P:V], last[:])
-                    else:
-                        nc.vector.tensor_copy(last[:], accs[m][:])
-                        nc.sync.dma_start(out_rows[:, m, P:V], last[:])
+                result = sb("result_sb%d_%d" % (half, m), [P, P], F32)
+                (nc.scalar.copy, nc.vector.tensor_copy)[m](result[:], acc[:])
+                queue = nc.scalar if (half, m) == (1, 0) else nc.sync
+                queue.dma_start(out_rows[:, m, half * P : (half + 1) * P], result[:])
 
-        own_term(0, 0)
-        own_term(0, 1)
-        own_term(1, 0)
+        own_term(0, 0, V)
+        own_term(1, 0, P)
+        own_term(1, P, V)
         finish_z(0)
-        own_term(1, 1)
-        second_product(0)
         finish_z(1)
+        second_product(0)
         second_product(1)

@@ -36,7 +36,7 @@ def tile_picked_lapl_none_e_kernel(
         psum = ctx.enter_context(tc.psum_pool(name="psum", bufs=1))
 
         def sb(name, shape, dtype, tag=None):
-            return keep.tile(shape, dtype, name=name, tag=tag or name, align_bytes=64)
+            return keep.tile(shape, dtype, name=name, tag=tag or name, align_bytes=256)
 
         def bank(number, name, shape):
             return psum.tile(shape, F32, name=name, tag="bank%d" % number)

@@ -78,24 +78,26 @@ def tile_picked_lapl_none_e_kernel(
 
         halves = [slice(half * SH, (half + 1) * SH) for half in range(2)]
         x_grouped = [sb("x_grouped%d" % half, [P, SH, PACK], BF16) for half in range(2)]
-        low = sb("low", [P, 2, S], BF16)
-        for j in range(2):
-            nc.vector.tensor_copy(low[:, j, :], x_slots[j][:].indirect(offs_sb[:]))
-        for grouped, nodes in zip(x_grouped, halves):
-            nc.scalar.copy(grouped[:, :, 0:2], low[:, :, nodes].rearrange("p j c -> p c j"))
-        high = sb("high", [P, 2, S], BF16)
-        nc.vector.tensor_copy(high[:, 0, :], x_slots[2][:].indirect(offs_sb[:]))
-        for nodes in halves:
+        x_pairs = sb("x_pairs", [P, PACK * S], BF16)[:].rearrange("p (h u c e) -> p h u c e", h=2, u=2, e=2)
+        for j in range(PACK - 1):
+            nc.vector.tensor_copy(x_pairs[:, :, j // 2, :, j % 2], x_slots[j][:].indirect(offs_sb[:]))
+        for half, nodes in enumerate(halves):
             entries = offs_sb[:, nodes.start // LANES : nodes.stop // LANES]
-            nc.vector.tensor_copy(high[:, 1, nodes], x_slots[3][:].indirect(entries))
-        for grouped, nodes in zip(x_grouped, halves):
-            nc.vector.tensor_copy(grouped[:, :, 2:4], high[:, :, nodes].rearrange("p j c -> p c j"))
+            nc.vector.tensor_copy(x_pairs[:, half, 1, :, 1], x_slots[3][:].indirect(entries))
+        for half, grouped in enumerate(x_grouped):
+            nc.vector.tensor_copy(
+                grouped[:].rearrange("p c (u e) -> p c u e", e=2), x_pairs[:, half].rearrange("p u c e -> p c u e")
+            )
 
         w1_mx, w1_paired = {}, {}
 
-        def deal_paired(side, engine_copy, tag):
+        def deal_paired(side, engine_copies, tag):
             w1_paired[side] = sb("w1_paired%d" % side, [P, P, PACK], BF16, tag)
-            engine_copy(w1_paired[side][:].rearrange("p (m e) j -> p m j e", e=2), w1_raw[side][:, :, :, 0:2])
+            dealt = w1_paired[side][:].rearrange("p (m e) j -> p m j e", e=2)
+            share = SIDE // len(engine_copies)
+            for n, engine_copy in enumerate(engine_copies):
+                groups = slice(n * share, (n + 1) * share)
+                engine_copy(dealt[:, groups, :, :], w1_raw[side][:, groups, :, 0:2])
 
         def quantize_paired(side):
             codes = sb("w1_codes%d" % side, [P, P], U32)
@@ -118,7 +120,7 @@ def tile_picked_lapl_none_e_kernel(
             for s in range(2):
                 w1_mx[2 + s] = (codes[:, s * P : (s + 1) * P], plane[:, s * P : (s + 1) * P])
 
-        deal_paired(0, nc.scalar.copy, None)
+        deal_paired(0, (nc.scalar.copy,), None)
         quantize_paired(0)
         deal_single(0, 0, SIDE, nc.scalar.copy)
         x_codes = [sb("x_codes0", [P, SH], U32), sb("x_codes1", [P, SH], U32, "w1_paired0")]
@@ -173,7 +175,7 @@ def tile_picked_lapl_none_e_kernel(
 
         deal_single(1, 0, SIDE // 2, nc.vector.tensor_copy)
         deal_single(1, SIDE // 2, SIDE, nc.scalar.copy)
-        deal_paired(1, nc.vector.tensor_copy, "x_grouped1")
+        deal_paired(1, (nc.vector.tensor_copy,), "x_grouped1")
         for number, (start, stop) in enumerate(PIECES):
             first_product(0, 2 + number, start, stop)
         quantize_single()

@@ -24,7 +24,7 @@ LANES = 16
 CEN = D
 SIDE = P // 2
 PIECES = ((0, SH), (SH, SH + P), (SH + P, S))
-EARLY = 3
+EARLY = 2
 
 
 def tile_picked_lapl_none_e_kernel(
@@ -33,10 +33,14 @@ def tile_picked_lapl_none_e_kernel(
     nc = tc.nc
     with ExitStack() as ctx:
         keep = ctx.enter_context(tc.tile_pool(name="keep", bufs=1))
+        placed = ctx.enter_context(tc.tile_pool(name="placed", bufs=1))
         psum = ctx.enter_context(tc.psum_pool(name="psum", bufs=1))
 
         def sb(name, shape, dtype, tag=None):
             return keep.tile(shape, dtype, name=name, tag=tag or name, align_bytes=256)
+
+        def sb_at(name, shape, dtype, offset):
+            return placed.tile(shape, dtype, name=name, offset=offset, align_bytes=256)
 
         def bank(number, name, shape):
             return psum.tile(shape, F32, name=name, tag="bank%d" % number)
@@ -89,60 +93,57 @@ def tile_picked_lapl_none_e_kernel(
                 grouped[:].rearrange("p c (u e) -> p c u e", e=2), x_pairs[:, half].rearrange("p u c e -> p c u e")
             )
 
-        w1_mx, w1_paired = {}, {}
+        paired_first = sb_at("paired_first", [P, P, PACK], BF16, 1024)
+        single_first = sb("single_first", [P, 2, SIDE, PACK], BF16)
+        codes_single = sb_at("codes_single", [P, 2, P], U32, 256)
+        plane_single = sb("plane_single", [P, 2, P], U8)
+        dealt_second = sb_at("dealt_second", [P, 2, P, PACK], BF16, 1792)
+        dealt_paired = [paired_first[:], dealt_second[:, 0]]
+        dealt_single = [single_first[:], dealt_second[:, 1].rearrange("p (s m) j -> p s m j", s=2)]
+        w1_mx = {2 + s: (codes_single[:, s, :], plane_single[:, s, :]) for s in range(2)}
 
-        def deal_paired(side, engine_copies, tag):
-            w1_paired[side] = sb("w1_paired%d" % side, [P, P, PACK], BF16, tag)
-            dealt = w1_paired[side][:].rearrange("p (m e) j -> p m j e", e=2)
-            share = SIDE // len(engine_copies)
-            for n, engine_copy in enumerate(engine_copies):
-                groups = slice(n * share, (n + 1) * share)
-                engine_copy(dealt[:, groups, :, :], w1_raw[side][:, groups, :, 0:2])
+        def deal_paired(side, engine_copy):
+            engine_copy(dealt_paired[side].rearrange("p (m e) j -> p m j e", e=2), w1_raw[side][:, :, :, 0:2])
+
+        def deal_single(side, engine_copy):
+            engine_copy(dealt_single[side].rearrange("p s m j -> p m j s"), w1_raw[side][:, :, :, 2:4])
 
         def quantize_paired(side):
             codes = sb("w1_codes%d" % side, [P, P], U32)
             plane = sb("w1_plane%d" % side, [P, P], U8)
-            nc.vector.quantize_mx(codes[:].bitcast(FP8X4), plane[:], w1_paired[side][:].rearrange("p c j -> p (c j)"))
+            nc.vector.quantize_mx(codes[:].bitcast(FP8X4), plane[:], dealt_paired[side].rearrange("p c j -> p (c j)"))
             w1_mx[side] = (codes[:], plane[:])
 
-        w1_single = sb("w1_single", [P, 2, P, PACK], BF16)
-
-        def deal_single(side, start, stop, engine_copy):
-            engine_copy(
-                w1_single[:, :, SIDE * side + start : SIDE * side + stop, :].rearrange("p s m j -> p m j s"),
-                w1_raw[side][:, start:stop, :, 2:4],
-            )
-
-        def quantize_single():
-            codes = sb("w1_codes_single", [P, 2 * P], U32)
-            plane = sb("w1_plane_single", [P, 2 * P], U8)
-            nc.vector.quantize_mx(codes[:].bitcast(FP8X4), plane[:], w1_single[:].rearrange("p s c j -> p (s c j)"))
+        def quantize_single(side):
+            cols = slice(SIDE * side, SIDE * (side + 1))
             for s in range(2):
-                w1_mx[2 + s] = (codes[:, s * P : (s + 1) * P], plane[:, s * P : (s + 1) * P])
+                nc.vector.quantize_mx(
+                    codes_single[:, s, cols].bitcast(FP8X4), plane_single[:, s, cols],
+                    dealt_single[side][:, s].rearrange("p m j -> p (m j)"),
+                )
 
-        deal_paired(0, (nc.scalar.copy,), None)
+        deal_paired(0, nc.scalar.copy)
         quantize_paired(0)
-        deal_single(0, 0, SIDE, nc.scalar.copy)
-        x_codes = [sb("x_codes0", [P, SH], U32), sb("x_codes1", [P, SH], U32, "w1_paired0")]
-        x_planes = [sb("x_plane%d" % half, [P, SH], U8) for half in range(2)]
-        x_mx = []
+        deal_single(0, nc.scalar.copy)
+        x_codes = [sb("x_codes%d" % half, [P, SH], U32) for half in range(2)]
+        x_planes = [sb("x_plane0", [P, SH], U8), sb_at("x_plane1", [P, SH], U8, 1280)]
         for start, stop in PIECES:
             half, cols = start // SH, slice(start % SH, start % SH + stop - start)
             codes, plane = x_codes[half][:, cols], x_planes[half][:, cols]
             nc.vector.quantize_mx(codes.bitcast(FP8X4), plane, x_grouped[half][:, cols, :].rearrange("p c j -> p (c j)"))
-            x_mx.append((codes, plane))
 
         h = [sb("h%d" % t, [P, S], F32) for t in range(PACK)]
 
         def first_product(t, number, start, stop):
             acc = bank(number, "acc%d_%d" % (t, start), [P, stop - start])
             codes, plane = w1_mx[t]
-            for (first, last), (piece_codes, piece_plane) in zip(PIECES, x_mx):
-                if start <= first and last <= stop:
-                    nc.tensor.matmul_mx(
-                        acc[:, first - start : last - start], codes.bitcast(FP8X4), plane,
-                        piece_codes.bitcast(FP8X4), piece_plane, start=True, stop=True,
-                    )
+            for first in range(start, stop, SH):
+                last = min(first + SH, stop)
+                half, cols = first // SH, slice(first % SH, first % SH + last - first)
+                nc.tensor.matmul_mx(
+                    acc[:, first - start : last - start], codes.bitcast(FP8X4), plane,
+                    x_codes[half][:, cols].bitcast(FP8X4), x_planes[half][:, cols], start=True, stop=True,
+                )
             nc.scalar.copy(h[t][:, start:stop], acc[:])
 
         def summed_terms(t, order, first_bank, terms):
@@ -173,16 +174,16 @@ def tile_picked_lapl_none_e_kernel(
                 nc.scalar.copy(staged[:], sums[half][:])
                 nc.tensor.transpose(pulls[half][:, s, :], staged[:], ident[:])
 
-        deal_single(1, 0, SIDE // 2, nc.vector.tensor_copy)
-        deal_single(1, SIDE // 2, SIDE, nc.scalar.copy)
-        deal_paired(1, (nc.vector.tensor_copy,), "x_grouped1")
-        for number, (start, stop) in enumerate(PIECES):
-            first_product(0, 2 + number, start, stop)
-        quantize_single()
+        deal_paired(1, nc.vector.tensor_copy)
+        deal_single(1, nc.vector.tensor_copy)
+        for number, start in enumerate(range(0, S, P)):
+            first_product(0, 2 + number, start, start + P)
         quantize_paired(1)
+        quantize_single(0)
+        quantize_single(1)
         terms_early = sb("terms_early", [P, EARLY, V], F32)
         terms_late = sb("terms_late", [P, D + 1 - EARLY, V], F32)
-        first_product(1, 5, 0, S)
+        first_product(1, 0, 0, S)
         paired_tile(0, 6, [terms_early[:, n, :] for n in range(EARLY)] + [terms_late[:, n, :] for n in range(D + 1 - EARLY)])
         first_product(2, 3, 0, S)
         first_product(3, 2, 0, S)

@@ -24,7 +24,7 @@ LANES = 16
 CEN = D
 SIDE = P // 2
 PIECES = ((0, SH), (SH, SH + P), (SH + P, S))
-EARLY = 2
+EARLY = 3
 
 
 def tile_picked_lapl_none_e_kernel(
@@ -66,13 +66,17 @@ def tile_picked_lapl_none_e_kernel(
             nc.sync.dma_start(raw[:], w1_rows[:, :, side * H // 2 : (side + 1) * H // 2])
             w1_raw.append(raw[:].rearrange("p j (m f) -> p m j f", f=PACK))
         lists, factors = {}, {CEN: minus_one[:]}
+        gate_first = sb("gate_first", [P, V], F32)
+        gate_rest = sb("gate_rest", [P, D - 1, V], F32)
         for u, name, source in ((CEN, "cen", cen), (0, "pos1", pos1), (1, "pos2", pos2), (2, "pos3", pos3), (3, "pos4", pos4)):
             lists[u] = sb(name + "_sb", [P, V // LANES], U16)
             nc.sync.dma_start(lists[u][:], source)
-        gate_sb = sb("gate_sb", [P, D, V], F32)
-        nc.sync.dma_start(gate_sb[:], gate.rearrange("d p v -> p d v"))
-        for u in range(D):
-            factors[u] = gate_sb[:, u, :]
+            if u == 0:
+                nc.sync.dma_start(gate_first[:], gate[0])
+        nc.sync.dma_start(gate_rest[:], gate[1:].rearrange("d p v -> p d v"))
+        factors[0] = gate_first[:]
+        for u in range(1, D):
+            factors[u] = gate_rest[:, u - 1, :]
         w2_codes = sb("w2_codes", [P, N], U32)
         nc.sync.dma_start(w2_codes[:].bitcast(I32), w2_words[0].rearrange("p n t -> p (n t)").bitcast(I32))
         for r in range(4):
@@ -97,9 +101,10 @@ def tile_picked_lapl_none_e_kernel(
         single_first = sb("single_first", [P, 2, SIDE, PACK], BF16)
         codes_single = sb_at("codes_single", [P, 2, P], U32, 256)
         plane_single = sb("plane_single", [P, 2, P], U8)
-        dealt_second = sb_at("dealt_second", [P, 2, P, PACK], BF16, 1792)
-        dealt_paired = [paired_first[:], dealt_second[:, 0]]
-        dealt_single = [single_first[:], dealt_second[:, 1].rearrange("p (s m) j -> p s m j", s=2)]
+        single_second = sb_at("single_second", [P, 2, SIDE, PACK], BF16, 1792)
+        paired_second = sb("paired_second", [P, P, PACK], BF16, "w1_codes0")
+        dealt_paired = [paired_first[:], paired_second[:]]
+        dealt_single = [single_first[:], single_second[:]]
         w1_mx = {2 + s: (codes_single[:, s, :], plane_single[:, s, :]) for s in range(2)}
 
         def deal_paired(side, engine_copy):
@@ -168,41 +173,44 @@ def tile_picked_lapl_none_e_kernel(
                 )
 
         def single_tile(s, first_bank, terms, pulls):
-            sums = summed_terms(2 + s, list(range(D - 1)), first_bank, terms)
+            sums = summed_terms(2 + s, list(range(1, D)), first_bank, terms)
             for half in range(2):
                 staged = sb("staged%d_%d" % (s, half), [P, P], F32)
                 nc.scalar.copy(staged[:], sums[half][:])
                 nc.tensor.transpose(pulls[half][:, s, :], staged[:], ident[:])
 
-        deal_paired(1, nc.vector.tensor_copy)
         deal_single(1, nc.vector.tensor_copy)
         for number, start in enumerate(range(0, S, P)):
             first_product(0, 2 + number, start, start + P)
-        quantize_paired(1)
         quantize_single(0)
         quantize_single(1)
-        terms_early = sb("terms_early", [P, EARLY, V], F32)
-        terms_late = sb("terms_late", [P, D + 1 - EARLY, V], F32)
-        first_product(1, 0, 0, S)
+        deal_paired(1, nc.scalar.copy)
+        first_product(2, 2, 0, S)
+        first_product(3, 3, 0, S)
+        base, term = 4096, 4 * V
+        terms_early = sb_at("terms_early", [P, EARLY, V], F32, base + 3 * term)
+        terms_late = sb_at("terms_late", [P, D + 1 - EARLY, V], F32, base + 6 * term)
         paired_tile(0, 6, [terms_early[:, n, :] for n in range(EARLY)] + [terms_late[:, n, :] for n in range(D + 1 - EARLY)])
-        first_product(2, 3, 0, S)
-        first_product(3, 2, 0, S)
-        terms_second = sb("terms_second", [P, D + 1, V], F32, "terms_early")
-        paired_tile(1, 0, [terms_second[:, n, :] for n in range(D + 1)])
+        quantize_paired(1)
+        first_product(1, 4, 0, S)
+        pulls = [bank((3, 5)[half], "pulls%d" % half, [P, 2, P]) for half in range(2)]
+        terms_two = sb("terms_two", [P, D - 1, V], F32)
+        single_tile(0, 0, [terms_two[:, n, :] for n in range(D - 1)], pulls)
+        terms_one_early = sb_at("terms_one_early", [P, 2, V], F32, base + 7 * term)
+        terms_one_late = sb_at("terms_one_late", [P, 3, V], F32, base + 4 * term)
+        paired_tile(1, 6, [terms_one_early[:, n, :] for n in range(2)] + [terms_one_late[:, n, :] for n in range(3)])
         z_grouped = [sb("z_grouped%d" % half, [P, P, PACK], BF16) for half in range(2)]
         for half in range(2):
             back = bank((2, 4)[half], "back%d" % half, [P, P])
             nc.tensor.transpose(back[:], z_pairs[half][:].rearrange("p m e -> p (m e)").bitcast(F32), ident[:])
             words = z_grouped[half][:].rearrange("p v j -> p (v j)").bitcast(F32).rearrange("p (v u) -> p v u", u=2)
             nc.scalar.copy(words[:, :, 0], back[:])
-        pulls = [bank((3, 5)[half], "pulls%d" % half, [P, 2, P]) for half in range(2)]
-        terms_single = sb("terms_single", [P, 2, D, V], F32, "terms_late")
-        single_tile(0, 6, [terms_single[:, 0, n, :] for n in range(D - 1)], pulls)
-        single_tile(1, 0, [terms_single[:, 1, n, :] for n in range(D - 1)], pulls)
+        terms_three = sb_at("terms_three", [P, D + 1, V], F32, base + 8 * term)
+        single_tile(1, 0, [terms_three[:, n, :] for n in range(D - 1)], pulls)
 
-        kept = terms_single[:, :, D - 1, :]
+        kept = terms_three[:, D - 1 :, :]
         for s in range(2):
-            nc.vector.tensor_tensor(kept[:, s, :], h[2 + s][:].indirect(lists[D - 1][:]), factors[D - 1], MULT)
+            nc.vector.tensor_tensor(kept[:, s, :], h[2 + s][:].indirect(lists[0][:]), factors[0], MULT)
         own = sb("own", [P, 2, V], F32)
 
         def own_term(s, start, stop):

@@ -15,16 +15,15 @@ U8 = mybir.dt.uint8
 FP8X4 = mybir.dt.float8_e4m3fn_x4
 COPY = mybir.ActivationFunctionType.Copy
 MULT = mybir.AluOpType.mult
-SUBTRACT = mybir.AluOpType.subtract
 
 P = 128
 PACK = 4
-SH = S // 2
+TILES = H // P
 LANES = 16
-CEN = D
-SIDE = P // 2
-PIECES = ((0, SH), (SH, SH + P), (SH + P, S))
-EARLY = 3
+LAST = D - 1
+RUN = D * V // P
+SV = 384
+PIECES = ((0, 256), (256, SV), (SV, S))
 
 
 def tile_picked_lapl_none_e_kernel(
@@ -47,36 +46,35 @@ def tile_picked_lapl_none_e_kernel(
 
         ident = sb("ident", [P, P], F32)
         make_identity(nc, ident[:])
-        minus_one = sb("minus_one", [P, V], F32)
-        nc.vector.memset(minus_one[:], -1.0)
         w2_plane = sb("w2_plane", [P, N], U8)
         nc.gpsimd.memset(w2_plane[:], 0)
 
         x_rows = xT.rearrange("(p j) t -> j p t", j=PACK)
-        x_slots = [sb("x_slot%d" % j, [P, T], F32) for j in range(PACK)]
+        x_slots = [sb_at("x_slot%d" % j, [P, T], F32, 4 * T * j) for j in range(PACK)]
         offs_sb = sb("offs_sb", [P, S // LANES], U16)
+        gate_runs = sb("gate_runs", [P, RUN], F32)
+        nc.sync.dma_start(gate_runs[:], gate.rearrange("d p (a b) -> (d p a) b", b=RUN)[:: P + 1, :])
         nc.sync.dma_start(x_slots[0][:], x_rows[0])
         nc.sync.dma_start(offs_sb[:], offs)
         for j in range(1, PACK):
             nc.sync.dma_start(x_slots[j][:], x_rows[j])
         w1_rows = w1.rearrange("(p j) c -> p j c", j=PACK)
-        w1_raw = []
-        for side in range(2):
-            raw = sb("w1_raw%d" % side, [P, PACK, H // 2], F32)
-            nc.sync.dma_start(raw[:], w1_rows[:, :, side * H // 2 : (side + 1) * H // 2])
-            w1_raw.append(raw[:].rearrange("p j (m f) -> p m j f", f=PACK))
-        lists, factors = {}, {CEN: minus_one[:]}
-        gate_first = sb("gate_first", [P, V], F32)
-        gate_rest = sb("gate_rest", [P, D - 1, V], F32)
-        for u, name, source in ((CEN, "cen", cen), (0, "pos1", pos1), (1, "pos2", pos2), (2, "pos3", pos3), (3, "pos4", pos4)):
-            lists[u] = sb(name + "_sb", [P, V // LANES], U16)
-            nc.sync.dma_start(lists[u][:], source)
-            if u == 0:
-                nc.sync.dma_start(gate_first[:], gate[0])
-        nc.sync.dma_start(gate_rest[:], gate[1:].rearrange("d p v -> p d v"))
-        factors[0] = gate_first[:]
-        for u in range(1, D):
-            factors[u] = gate_rest[:, u - 1, :]
+        w1_raw = [sb("w1_raw%d" % t, [P, PACK, P], F32) for t in range(TILES)]
+        cen_sb = sb("cen_sb", [P, V // LANES], U16)
+        pos_sb = [sb("pos_sb%d" % u, [P, V // LANES], U16) for u in range(D)]
+        gate_sb = sb("gate_sb", [P, D, V], F32)
+        gates = [gate_sb[:, u, :] for u in range(D)]
+        pos = (pos1, pos2, pos3, pos4)
+
+        def load_w1(t):
+            nc.sync.dma_start(w1_raw[t][:], w1_rows[:, :, t * P : (t + 1) * P])
+
+        load_w1(0)
+        nc.sync.dma_start(pos_sb[LAST][:], pos[LAST])
+        nc.sync.dma_start(cen_sb[:], cen)
+        for u in range(LAST):
+            load_w1(u + 1)
+            nc.sync.dma_start(pos_sb[u][:], pos[u])
         w2_codes = sb("w2_codes", [P, N], U32)
         nc.sync.dma_start(w2_codes[:].bitcast(I32), w2_words[0].rearrange("p n t -> p (n t)").bitcast(I32))
         for r in range(4):
@@ -84,171 +82,157 @@ def tile_picked_lapl_none_e_kernel(
                 w2_plane[32 * r : 32 * r + 4, :].bitcast(I32), w2_scales[0, 4 * r : 4 * r + 4, :].bitcast(I32)
             )
 
-        halves = [slice(half * SH, (half + 1) * SH) for half in range(2)]
-        x_grouped = [sb("x_grouped%d" % half, [P, SH, PACK], BF16) for half in range(2)]
-        x_pairs = sb("x_pairs", [P, PACK * S], BF16)[:].rearrange("p (h u c e) -> p h u c e", h=2, u=2, e=2)
-        for j in range(PACK - 1):
-            nc.vector.tensor_copy(x_pairs[:, :, j // 2, :, j % 2], x_slots[j][:].indirect(offs_sb[:]))
-        for half, nodes in enumerate(halves):
-            entries = offs_sb[:, nodes.start // LANES : nodes.stop // LANES]
-            nc.vector.tensor_copy(x_pairs[:, half, 1, :, 1], x_slots[3][:].indirect(entries))
-        for half, grouped in enumerate(x_grouped):
-            nc.vector.tensor_copy(
-                grouped[:].rearrange("p c (u e) -> p c u e", e=2), x_pairs[:, half].rearrange("p u c e -> p c u e")
+        minus_runs = sb_at("minus_runs", [P, RUN], F32, 4 * T * PACK)
+        nc.scalar.activation(minus_runs[:], gate_runs[:], COPY, scale=-1.0)
+        spread = gate_sb[:].rearrange("p d (q g b) -> p g (d q) b", g=2, b=RUN // 2)
+        for g in range(2):
+            rows = bank(4 + g, "gate_rows%d" % g, [P, RUN // 2, P])
+            for b in range(RUN // 2):
+                column = g * RUN // 2 + b
+                nc.tensor.transpose(rows[:, b, :], minus_runs[:, column : column + 1].to_broadcast([P, P]), ident[:])
+            nc.scalar.copy(spread[:, g], rows[:].rearrange("p b n -> p n b"))
+
+        x_pairs = sb("x_pairs", [P, PACK * SV], BF16)[:].rearrange("p (u c e) -> p u c e", u=2, e=2)
+        x_planes = sb_at("x_planes", [P, PACK * (S - SV)], BF16, 4 * T * PACK)[:].rearrange("p (j c) -> p j c", j=PACK)
+        for j in range(PACK):
+            nc.vector.tensor_copy(x_pairs[:, j // 2, :, j % 2], x_slots[j][:].indirect(offs_sb[:, : SV // LANES]))
+            nc.scalar.activation(x_planes[:, j, :], x_slots[j][:].indirect(offs_sb[:, SV // LANES :]), COPY)
+        grouped_v = sb("grouped_v", [P, SV, PACK], BF16)
+        grouped_s = sb("grouped_s", [P, S - SV, PACK], BF16)
+
+        dealt = [sb_at("dealt%d" % t, [P, P, PACK], BF16, 4 * T * (2 if t == 0 else 3) + T * t) for t in range(TILES)]
+        w1_codes = [sb("w1_codes%d" % t, [P, P], U32) for t in range(TILES)]
+        w1_planes = [sb("w1_plane%d" % t, [P, P], U8) for t in range(TILES)]
+
+        def deal(t, engine_copy):
+            engine_copy(
+                dealt[t][:].rearrange("p (c i) j -> p c j i", i=4), w1_raw[t][:].rearrange("p j (c i) -> p c j i", i=4)
             )
 
-        paired_first = sb_at("paired_first", [P, P, PACK], BF16, 1024)
-        single_first = sb("single_first", [P, 2, SIDE, PACK], BF16)
-        codes_single = sb_at("codes_single", [P, 2, P], U32, 256)
-        plane_single = sb("plane_single", [P, 2, P], U8)
-        single_second = sb_at("single_second", [P, 2, SIDE, PACK], BF16, 1792)
-        paired_second = sb("paired_second", [P, P, PACK], BF16, "w1_codes0")
-        dealt_paired = [paired_first[:], paired_second[:]]
-        dealt_single = [single_first[:], single_second[:]]
-        w1_mx = {2 + s: (codes_single[:, s, :], plane_single[:, s, :]) for s in range(2)}
+        def quantize_w1(t):
+            nc.vector.quantize_mx(w1_codes[t][:].bitcast(FP8X4), w1_planes[t][:], dealt[t][:].rearrange("p c j -> p (c j)"))
 
-        def deal_paired(side, engine_copy):
-            engine_copy(dealt_paired[side].rearrange("p (m e) j -> p m j e", e=2), w1_raw[side][:, :, :, 0:2])
+        deal(0, nc.scalar.copy)
+        nc.scalar.copy(
+            grouped_s[:].rearrange("p (c i) j -> p c j i", i=4), x_planes.rearrange("p j (c i) -> p c j i", i=4)
+        )
+        nc.vector.tensor_copy(
+            grouped_v[:].rearrange("p c (u e) -> p c u e", e=2), x_pairs.rearrange("p u c e -> p c u e")
+        )
+        x_mx = []
+        for n, (start, stop) in enumerate(PIECES):
+            codes = sb("x_codes%d" % n, [P, stop - start], U32)
+            if n == 1:
+                quantize_w1(0)
+                plane = sb_at("x_plane1", [P, stop - start], U8, 4 * T * 2)
+            else:
+                plane = sb("x_plane%d" % n, [P, stop - start], U8)
+            source = grouped_v[:, start:stop, :] if stop <= SV else grouped_s[:]
+            nc.vector.quantize_mx(codes[:].bitcast(FP8X4), plane[:], source.rearrange("p c j -> p (c j)"))
+            x_mx.append((codes, plane))
 
-        def deal_single(side, engine_copy):
-            engine_copy(dealt_single[side].rearrange("p s m j -> p m j s"), w1_raw[side][:, :, :, 2:4])
+        h = [sb("h%d" % t, [P, S], F32) for t in range(TILES)]
 
-        def quantize_paired(side):
-            codes = sb("w1_codes%d" % side, [P, P], U32)
-            plane = sb("w1_plane%d" % side, [P, P], U8)
-            nc.vector.quantize_mx(codes[:].bitcast(FP8X4), plane[:], dealt_paired[side].rearrange("p c j -> p (c j)"))
-            w1_mx[side] = (codes[:], plane[:])
-
-        def quantize_single(side):
-            cols = slice(SIDE * side, SIDE * (side + 1))
-            for s in range(2):
-                nc.vector.quantize_mx(
-                    codes_single[:, s, cols].bitcast(FP8X4), plane_single[:, s, cols],
-                    dealt_single[side][:, s].rearrange("p m j -> p (m j)"),
-                )
-
-        deal_paired(0, nc.scalar.copy)
-        quantize_paired(0)
-        deal_single(0, nc.scalar.copy)
-        x_codes = [sb("x_codes%d" % half, [P, SH], U32) for half in range(2)]
-        x_planes = [sb("x_plane0", [P, SH], U8), sb_at("x_plane1", [P, SH], U8, 1280)]
-        for start, stop in PIECES:
-            half, cols = start // SH, slice(start % SH, start % SH + stop - start)
-            codes, plane = x_codes[half][:, cols], x_planes[half][:, cols]
-            nc.vector.quantize_mx(codes.bitcast(FP8X4), plane, x_grouped[half][:, cols, :].rearrange("p c j -> p (c j)"))
-
-        h = [sb("h%d" % t, [P, S], F32) for t in range(PACK)]
-
-        def first_product(t, number, start, stop):
+        def first_product(t, number, start, stop, engine_copy):
             acc = bank(number, "acc%d_%d" % (t, start), [P, stop - start])
-            codes, plane = w1_mx[t]
-            for first in range(start, stop, SH):
-                last = min(first + SH, stop)
-                half, cols = first // SH, slice(first % SH, first % SH + last - first)
-                nc.tensor.matmul_mx(
-                    acc[:, first - start : last - start], codes.bitcast(FP8X4), plane,
-                    x_codes[half][:, cols].bitcast(FP8X4), x_planes[half][:, cols], start=True, stop=True,
-                )
-            nc.scalar.copy(h[t][:, start:stop], acc[:])
-
-        def summed_terms(t, order, first_bank, terms):
-            sums = [bank(first_bank + half, "sum%d_%d" % (t, half), [P, P]) for half in range(2)]
-            for n, u in enumerate(order):
-                nc.vector.tensor_tensor(terms[n], h[t][:].indirect(lists[u][:]), factors[u], MULT)
-                for half in range(2):
-                    nc.tensor.matmul(
-                        sums[half][:], terms[n][:, half * P : (half + 1) * P], ident[:],
-                        start=(n == 0), stop=(n == len(order) - 1), is_transpose=True,
+            for (first, last), (codes, plane) in zip(PIECES, x_mx):
+                if start <= first and last <= stop:
+                    nc.tensor.matmul_mx(
+                        acc[:, first - start : last - start], w1_codes[t][:].bitcast(FP8X4), w1_planes[t][:],
+                        codes[:].bitcast(FP8X4), plane[:], start=True, stop=True,
                     )
-            return sums
+            engine_copy(h[t][:, start:stop], acc[:])
 
-        z_pairs = [sb("z_pairs%d" % half, [P, P, 2], BF16) for half in range(2)]
+        deal(1, nc.scalar.copy)
+        deal(2, nc.scalar.copy)
+        for number, (start, stop) in enumerate(PIECES):
+            first_product(0, number, start, stop, nc.scalar.copy if number else nc.vector.tensor_copy)
+        quantize_w1(1)
+        quantize_w1(2)
 
-        def paired_tile(side, first_bank, terms):
-            sums = summed_terms(side, [CEN] + list(range(D)), first_bank, terms)
-            for half in range(2):
-                nc.scalar.activation(
-                    z_pairs[half][:, SIDE * side : SIDE * (side + 1), :].rearrange("p m e -> p (m e)"), sums[half][:],
-                    COPY, scale=-1.0,
+        turned = [sb("turned%d" % half, [P, 2, P, 2], BF16) for half in range(2)]
+        sums = {}
+
+        def add_turned(t, term, first, last, halves=(0, 1)):
+            for half in halves:
+                nc.tensor.matmul(
+                    sums[t][half][:], term[:, half * P : (half + 1) * P], ident[:],
+                    start=first, stop=last, is_transpose=True,
                 )
 
-        def single_tile(s, first_bank, terms, pulls):
-            sums = summed_terms(2 + s, list(range(1, D)), first_bank, terms)
+        def scalar_terms(t):
+            sums[t] = [bank(4 + 2 * (t % 2) + half, "sum%d_%d" % (t, half), [P, P]) for half in range(2)]
+            raw = sb("raw%d" % t, [P, V], F32)
+            own = sb("own%d" % t, [P, V], F32)
+            nc.scalar.activation(raw[:], h[t][:].indirect(pos_sb[LAST][:]), COPY)
+            nc.scalar.activation(own[:], h[t][:].indirect(cen_sb[:]), COPY)
+            return raw, own
+
+        def vector_terms(t, raw, own):
+            terms = sb("terms%d" % t, [P, D, V], F32)
+            for u in range(LAST - 1):
+                nc.vector.tensor_tensor(terms[:, u, :], h[t][:].indirect(pos_sb[u][:]), gates[u], MULT)
+                add_turned(t, terms[:, u, :], u == 0, False)
+            add_turned(t, own[:], False, False)
+            nc.vector.tensor_tensor(terms[:, LAST, :], raw[:], gates[LAST], MULT)
+            add_turned(t, terms[:, LAST, :], False, False)
+            u = LAST - 1
+            for halves in ((0,), (1,)) if t == TILES - 1 else ((0, 1),):
+                start, stop = halves[0] * P, (halves[-1] + 1) * P
+                entries = pos_sb[u][:, start // LANES : stop // LANES]
+                nc.vector.tensor_tensor(terms[:, u, start:stop], h[t][:].indirect(entries), gates[u][:, start:stop], MULT)
+                add_turned(t, terms[:, u, :], False, True, halves)
+
+        def cast(t):
+            part = slice(32 * t, 32 * (t + 1))
             for half in range(2):
-                staged = sb("staged%d_%d" % (s, half), [P, P], F32)
-                nc.scalar.copy(staged[:], sums[half][:])
-                nc.tensor.transpose(pulls[half][:, s, :], staged[:], ident[:])
+                engine_copy = nc.vector.tensor_copy if (t, half) == (TILES - 1, 1) else nc.scalar.copy
+                engine_copy(turned[half][:, :, part, :], sums[t][half][:].rearrange("v (q u e) -> v u q e", u=2, e=2))
 
-        deal_single(1, nc.vector.tensor_copy)
-        for number, start in enumerate(range(0, S, P)):
-            first_product(0, 2 + number, start, start + P)
-        quantize_single(0)
-        quantize_single(1)
-        deal_paired(1, nc.scalar.copy)
-        first_product(2, 2, 0, S)
-        first_product(3, 3, 0, S)
-        base, term = 4096, 4 * V
-        terms_early = sb_at("terms_early", [P, EARLY, V], F32, base + 3 * term)
-        terms_late = sb_at("terms_late", [P, D + 1 - EARLY, V], F32, base + 6 * term)
-        paired_tile(0, 6, [terms_early[:, n, :] for n in range(EARLY)] + [terms_late[:, n, :] for n in range(D + 1 - EARLY)])
-        quantize_paired(1)
-        first_product(1, 4, 0, S)
-        pulls = [bank((3, 5)[half], "pulls%d" % half, [P, 2, P]) for half in range(2)]
-        terms_two = sb("terms_two", [P, D - 1, V], F32)
-        single_tile(0, 0, [terms_two[:, n, :] for n in range(D - 1)], pulls)
-        terms_one_early = sb_at("terms_one_early", [P, 2, V], F32, base + 7 * term)
-        terms_one_late = sb_at("terms_one_late", [P, 3, V], F32, base + 4 * term)
-        paired_tile(1, 6, [terms_one_early[:, n, :] for n in range(2)] + [terms_one_late[:, n, :] for n in range(3)])
-        z_grouped = [sb("z_grouped%d" % half, [P, P, PACK], BF16) for half in range(2)]
-        for half in range(2):
-            back = bank((2, 4)[half], "back%d" % half, [P, P])
-            nc.tensor.transpose(back[:], z_pairs[half][:].rearrange("p m e -> p (m e)").bitcast(F32), ident[:])
-            words = z_grouped[half][:].rearrange("p v j -> p (v j)").bitcast(F32).rearrange("p (v u) -> p v u", u=2)
-            nc.scalar.copy(words[:, :, 0], back[:])
-        terms_three = sb_at("terms_three", [P, D + 1, V], F32, base + 8 * term)
-        single_tile(1, 0, [terms_three[:, n, :] for n in range(D - 1)], pulls)
-
-        kept = terms_three[:, D - 1 :, :]
-        for s in range(2):
-            nc.vector.tensor_tensor(kept[:, s, :], h[2 + s][:].indirect(lists[0][:]), factors[0], MULT)
-        own = sb("own", [P, 2, V], F32)
-
-        def own_term(s, start, stop):
-            entries = lists[CEN][:, start // LANES : stop // LANES]
-            nc.vector.tensor_tensor(
-                own[:, s, start:stop], h[2 + s][:].indirect(entries), kept[:, s, start:stop], SUBTRACT
-            )
-
-        def finish_z(half):
-            nc.vector.tensor_tensor(
-                z_grouped[half][:, :, 2:4], own[:, :, half * P : (half + 1) * P].rearrange("p s v -> p v s"),
-                pulls[half][:].rearrange("p s v -> p v s"), SUBTRACT,
-            )
+        fetched = scalar_terms(0)
+        first_product(1, 3, 0, S, nc.scalar.copy)
+        deal(3, nc.scalar.copy)
+        vector_terms(0, *fetched)
+        quantize_w1(3)
+        fetched = scalar_terms(1)
+        first_product(2, 0, 0, S, nc.scalar.copy)
+        cast(0)
+        vector_terms(1, *fetched)
+        fetched = scalar_terms(2)
+        first_product(3, 1, 0, S, nc.scalar.copy)
+        cast(1)
+        vector_terms(2, *fetched)
+        fetched = scalar_terms(3)
+        cast(2)
+        vector_terms(3, *fetched)
+        cast(3)
 
         out_rows = out.rearrange("(m p) v -> p m v", p=P)
-
-        def second_product(half):
+        copies = (nc.scalar.copy, nc.vector.tensor_copy)
+        z_grouped = [sb("z_grouped%d" % half, [P, P, PACK], BF16) for half in range(2)]
+        for half in range(2):
+            back = bank(2 + half, "back%d" % half, [P, 2, P])
+            words = turned[half][:].rearrange("v u p e -> v (u p e)").bitcast(F32)
+            for u in range(2):
+                nc.tensor.transpose(back[:, u, :], words[:, u * P : (u + 1) * P], ident[:])
+            copies[half](
+                z_grouped[half][:].rearrange("p v j -> p (v j)").bitcast(F32).rearrange("p (v u) -> p v u", u=2),
+                back[:].rearrange("p u v -> p v u"),
+            )
+        for half in range(2):
             z_codes = sb("z_codes%d" % half, [P, P], U32)
             z_plane = sb("z_plane%d" % half, [P, P], U8)
             nc.vector.quantize_mx(
                 z_codes[:].bitcast(FP8X4), z_plane[:], z_grouped[half][:].rearrange("p v j -> p (v j)")
             )
             for m in range(2):
-                acc = bank((6, 7, 2, 4)[2 * half + m], "result%d_%d" % (half, m), [P, P])
+                acc = bank((0, 1, 4, 5)[2 * half + m], "result%d_%d" % (half, m), [P, P])
                 cols = slice(m * P, (m + 1) * P)
                 nc.tensor.matmul_mx(
                     acc[:], w2_codes[:, cols].bitcast(FP8X4), w2_plane[:, cols],
                     z_codes[:].bitcast(FP8X4), z_plane[:], start=True, stop=True,
                 )
                 result = sb("result_sb%d_%d" % (half, m), [P, P], F32)
-                (nc.scalar.copy, nc.vector.tensor_copy)[m](result[:], acc[:])
+                copies[m](result[:], acc[:])
                 queue = nc.scalar if (half, m) == (1, 0) else nc.sync
                 queue.dma_start(out_rows[:, m, half * P : (half + 1) * P], result[:])
-
-        own_term(0, 0, V)
-        own_term(1, 0, P)
-        own_term(1, P, V)
-        finish_z(0)
-        finish_z(1)
-        second_product(0)
-        second_product(1)

@@ -22,6 +22,7 @@ TILES = H // P
 LANES = 16
 LAST = D - 1
 RUN = D * V // P
+RAWS = (1, 1, 1, 2)
 SV = 384
 PIECES = ((0, 256), (256, SV), (SV, S))
 
@@ -151,67 +152,84 @@ def tile_picked_lapl_none_e_kernel(
         quantize_w1(2)
 
         turned = [sb("turned%d" % half, [P, 2, P, 2], BF16) for half in range(2)]
-        sums = {}
+        sums = [
+            [bank(first + half, "sum%d_%d" % (t, half), [P, P]) for half in range(2)]
+            for t, first in enumerate((4, 6, 2, 0))
+        ]
 
-        def add_turned(t, term, first, last, halves=(0, 1)):
+        added = {(t, half): 0 for t in range(TILES) for half in range(2)}
+
+        def add_turned(t, term, halves=(0, 1)):
             for half in halves:
                 nc.tensor.matmul(
                     sums[t][half][:], term[:, half * P : (half + 1) * P], ident[:],
-                    start=first, stop=last, is_transpose=True,
+                    start=added[t, half] == 0, stop=added[t, half] == D, is_transpose=True,
                 )
+                added[t, half] = added[t, half] + 1
 
-        def scalar_terms(t):
-            sums[t] = [bank(4 + 2 * (t % 2) + half, "sum%d_%d" % (t, half), [P, P]) for half in range(2)]
-            raw = sb("raw%d" % t, [P, V], F32)
-            own = sb("own%d" % t, [P, V], F32)
-            nc.scalar.activation(raw[:], h[t][:].indirect(pos_sb[LAST][:]), COPY)
-            nc.scalar.activation(own[:], h[t][:].indirect(cen_sb[:]), COPY)
-            return raw, own
+        raws = [sb("raw%d" % t, [P, count, V], F32) if count else None for t, count in enumerate(RAWS)]
+        owns = [sb("own%d" % t, [P, V], F32) for t in range(TILES)]
 
-        def vector_terms(t, raw, own):
-            terms = sb("terms%d" % t, [P, D, V], F32)
-            for u in range(LAST - 1):
-                nc.vector.tensor_tensor(terms[:, u, :], h[t][:].indirect(pos_sb[u][:]), gates[u], MULT)
-                add_turned(t, terms[:, u, :], u == 0, False)
-            add_turned(t, own[:], False, False)
-            nc.vector.tensor_tensor(terms[:, LAST, :], raw[:], gates[LAST], MULT)
-            add_turned(t, terms[:, LAST, :], False, False)
-            u = LAST - 1
-            for halves in ((0,), (1,)) if t == TILES - 1 else ((0, 1),):
-                start, stop = halves[0] * P, (halves[-1] + 1) * P
-                entries = pos_sb[u][:, start // LANES : stop // LANES]
-                nc.vector.tensor_tensor(terms[:, u, start:stop], h[t][:].indirect(entries), gates[u][:, start:stop], MULT)
-                add_turned(t, terms[:, u, :], False, True, halves)
+        def fetch_raw(t):
+            for n in range(RAWS[t]):
+                nc.scalar.activation(raws[t][:, n, :], h[t][:].indirect(pos_sb[D - RAWS[t] + n][:]), COPY)
+
+        def fetch_own(t):
+            nc.scalar.activation(owns[t][:], h[t][:].indirect(cen_sb[:]), COPY)
+
+        terms = [sb("terms%d" % t, [P, D, V], F32) for t in range(TILES)]
+
+        def fetch_weighted(t, u):
+            nc.vector.tensor_tensor(terms[t][:, u, :], h[t][:].indirect(pos_sb[u][:]), gates[u], MULT)
+            add_turned(t, terms[t][:, u, :])
+
+        def weigh(t, halves):
+            cols = slice(halves[0] * P, (halves[-1] + 1) * P)
+            first = D - RAWS[t]
+            nc.vector.tensor_tensor(terms[t][:, first:, cols], raws[t][:, :, cols], gate_sb[:, first:, cols], MULT)
+            for u in range(first, D):
+                add_turned(t, terms[t][:, u, :], halves)
 
         def cast(t):
             part = slice(32 * t, 32 * (t + 1))
             for half in range(2):
-                engine_copy = nc.vector.tensor_copy if (t, half) == (TILES - 1, 1) else nc.scalar.copy
+                engine_copy = nc.vector.tensor_copy if t == 2 or (t, half) == (3, 1) else nc.scalar.copy
                 engine_copy(turned[half][:, :, part, :], sums[t][half][:].rearrange("v (q u e) -> v u q e", u=2, e=2))
 
-        fetched = scalar_terms(0)
-        first_product(1, 3, 0, S, nc.scalar.copy)
-        deal(3, nc.scalar.copy)
-        vector_terms(0, *fetched)
-        quantize_w1(3)
-        fetched = scalar_terms(1)
-        first_product(2, 0, 0, S, nc.scalar.copy)
-        cast(0)
-        vector_terms(1, *fetched)
-        fetched = scalar_terms(2)
-        first_product(3, 1, 0, S, nc.scalar.copy)
+        def vector_terms(t):
+            fetch_weighted(t, 0)
+            fetch_weighted(t, 1)
+            add_turned(t, owns[t][:])
+            weigh(t, (0, 1))
+            fetch_weighted(t, 2)
+
+        for t in range(TILES - 1):
+            fetch_raw(t)
+            fetch_own(t)
+            first_product(t + 1, (3, 0, 1)[t], 0, S, nc.scalar.copy)
+            if t == 0:
+                deal(3, nc.scalar.copy)
+            if t == 1:
+                cast(0)
+            vector_terms(t)
+            if t == 0:
+                quantize_w1(3)
+        fetch_raw(3)
+        fetch_own(3)
         cast(1)
-        vector_terms(2, *fetched)
-        fetched = scalar_terms(3)
+        fetch_weighted(3, 0)
+        fetch_weighted(3, 1)
+        for half in range(2):
+            weigh(3, (half,))
+            add_turned(3, owns[3][:], (half,))
         cast(2)
-        vector_terms(3, *fetched)
         cast(3)
 
         out_rows = out.rearrange("(m p) v -> p m v", p=P)
         copies = (nc.scalar.copy, nc.vector.tensor_copy)
         z_grouped = [sb("z_grouped%d" % half, [P, P, PACK], BF16) for half in range(2)]
         for half in range(2):
-            back = bank(2 + half, "back%d" % half, [P, 2, P])
+            back = bank(4 + half, "back%d" % half, [P, 2, P])
             words = turned[half][:].rearrange("v u p e -> v (u p e)").bitcast(F32)
             for u in range(2):
                 nc.tensor.transpose(back[:, u, :], words[:, u * P : (u + 1) * P], ident[:])
@@ -226,7 +244,7 @@ def tile_picked_lapl_none_e_kernel(
                 z_codes[:].bitcast(FP8X4), z_plane[:], z_grouped[half][:].rearrange("p v j -> p (v j)")
             )
             for m in range(2):
-                acc = bank((0, 1, 4, 5)[2 * half + m], "result%d_%d" % (half, m), [P, P])
+                acc = bank((6, 7, 2, 3)[2 * half + m], "result%d_%d" % (half, m), [P, P])
                 cols = slice(m * P, (m + 1) * P)
                 nc.tensor.matmul_mx(
                     acc[:], w2_codes[:, cols].bitcast(FP8X4), w2_plane[:, cols],

@@ -120,28 +120,23 @@ def tile_picked_lapl_none_e_kernel(
         nc.vector.tensor_copy(
             grouped_v[:].rearrange("p c (u e) -> p c u e", e=2), x_pairs.rearrange("p u c e -> p c u e")
         )
-        x_mx = []
-        for n, (start, stop) in enumerate(PIECES):
-            codes = sb("x_codes%d" % n, [P, stop - start], U32)
-            if n == 1:
-                quantize_w1(0)
-                plane = sb_at("x_plane1", [P, stop - start], U8, 4 * T * 2)
-            else:
-                plane = sb("x_plane%d" % n, [P, stop - start], U8)
+        quantize_w1(0)
+        x_codes = sb("x_codes", [P, S], U32)
+        x_plane = sb_at("x_plane", [P, S], U8, 4 * T * 2)
+        for start, stop in PIECES:
             source = grouped_v[:, start:stop, :] if stop <= SV else grouped_s[:]
-            nc.vector.quantize_mx(codes[:].bitcast(FP8X4), plane[:], source.rearrange("p c j -> p (c j)"))
-            x_mx.append((codes, plane))
+            nc.vector.quantize_mx(
+                x_codes[:, start:stop].bitcast(FP8X4), x_plane[:, start:stop], source.rearrange("p c j -> p (c j)")
+            )
 
         h = [sb("h%d" % t, [P, S], F32) for t in range(TILES)]
 
         def first_product(t, number, start, stop, engine_copy):
             acc = bank(number, "acc%d_%d" % (t, start), [P, stop - start])
-            for (first, last), (codes, plane) in zip(PIECES, x_mx):
-                if start <= first and last <= stop:
-                    nc.tensor.matmul_mx(
-                        acc[:, first - start : last - start], w1_codes[t][:].bitcast(FP8X4), w1_planes[t][:],
-                        codes[:].bitcast(FP8X4), plane[:], start=True, stop=True,
-                    )
+            nc.tensor.matmul_mx(
+                acc[:], w1_codes[t][:].bitcast(FP8X4), w1_planes[t][:],
+                x_codes[:, start:stop].bitcast(FP8X4), x_plane[:, start:stop], start=True, stop=True,
+            )
             engine_copy(h[t][:, start:stop], acc[:])
 
         deal(1, nc.scalar.copy)

@@ -228,7 +228,7 @@ def tile_picked_lapl_none_e_kernel(
             words = turned[half][:].rearrange("v u p e -> v (u p e)").bitcast(F32)
             for u in range(2):
                 nc.tensor.transpose(back[:, u, :], words[:, u * P : (u + 1) * P], ident[:])
-            copies[half](
+            nc.scalar.copy(
                 z_grouped[half][:].rearrange("p v j -> p (v j)").bitcast(F32).rearrange("p (v u) -> p v u", u=2),
                 back[:].rearrange("p u v -> p v u"),
             )

@@ -20,11 +20,12 @@ P = 128
 PACK = 4
 TILES = H // P
 LANES = 16
-LAST = D - 1
 RUN = D * V // P
-RAWS = (1, 1, 1, 2)
-SV = 384
-PIECES = ((0, 256), (256, SV), (SV, S))
+RAWS = (1, 1, 2, 1)
+V_PIECES = ((0, 384),)
+X_AT = 8192
+S_PIECE = (384, 512)
+PIECES = ((0, 256), (256, 384), (384, 512))
 
 
 def tile_picked_lapl_none_e_kernel(
@@ -36,8 +37,8 @@ def tile_picked_lapl_none_e_kernel(
         placed = ctx.enter_context(tc.tile_pool(name="placed", bufs=1))
         psum = ctx.enter_context(tc.psum_pool(name="psum", bufs=1))
 
-        def sb(name, shape, dtype, tag=None):
-            return keep.tile(shape, dtype, name=name, tag=tag or name, align_bytes=256)
+        def sb(name, shape, dtype):
+            return keep.tile(shape, dtype, name=name, align_bytes=256)
 
         def sb_at(name, shape, dtype, offset):
             return placed.tile(shape, dtype, name=name, offset=offset, align_bytes=256)
@@ -51,7 +52,7 @@ def tile_picked_lapl_none_e_kernel(
         nc.gpsimd.memset(w2_plane[:], 0)
 
         x_rows = xT.rearrange("(p j) t -> j p t", j=PACK)
-        x_slots = [sb_at("x_slot%d" % j, [P, T], F32, 4 * T * j) for j in range(PACK)]
+        x_slots = [sb_at("x_slot%d" % j, [P, T], F32, X_AT + 4 * T * j) for j in range(PACK)]
         offs_sb = sb("offs_sb", [P, S // LANES], U16)
         gate_runs = sb("gate_runs", [P, RUN], F32)
         nc.sync.dma_start(gate_runs[:], gate.rearrange("d p (a b) -> (d p a) b", b=RUN)[:: P + 1, :])
@@ -64,18 +65,20 @@ def tile_picked_lapl_none_e_kernel(
         cen_sb = sb("cen_sb", [P, V // LANES], U16)
         pos_sb = [sb("pos_sb%d" % u, [P, V // LANES], U16) for u in range(D)]
         gate_sb = sb("gate_sb", [P, D, V], F32)
-        gates = [gate_sb[:, u, :] for u in range(D)]
         pos = (pos1, pos2, pos3, pos4)
 
         def load_w1(t):
             nc.sync.dma_start(w1_raw[t][:], w1_rows[:, :, t * P : (t + 1) * P])
 
         load_w1(0)
-        nc.sync.dma_start(pos_sb[LAST][:], pos[LAST])
+        nc.sync.dma_start(pos_sb[3][:], pos[3])
+        load_w1(1)
+        nc.sync.dma_start(pos_sb[0][:], pos[0])
+        nc.sync.dma_start(pos_sb[1][:], pos[1])
+        load_w1(2)
+        nc.sync.dma_start(pos_sb[2][:], pos[2])
+        load_w1(3)
         nc.sync.dma_start(cen_sb[:], cen)
-        for u in range(LAST):
-            load_w1(u + 1)
-            nc.sync.dma_start(pos_sb[u][:], pos[u])
         w2_codes = sb("w2_codes", [P, N], U32)
         nc.sync.dma_start(w2_codes[:].bitcast(I32), w2_words[0].rearrange("p n t -> p (n t)").bitcast(I32))
         for r in range(4):
@@ -83,87 +86,110 @@ def tile_picked_lapl_none_e_kernel(
                 w2_plane[32 * r : 32 * r + 4, :].bitcast(I32), w2_scales[0, 4 * r : 4 * r + 4, :].bitcast(I32)
             )
 
-        minus_runs = sb_at("minus_runs", [P, RUN], F32, 4 * T * PACK)
+        minus_runs = sb_at("minus_runs", [P, RUN], F32, 0)
         nc.scalar.activation(minus_runs[:], gate_runs[:], COPY, scale=-1.0)
         spread = gate_sb[:].rearrange("p d (q g b) -> p g (d q) b", g=2, b=RUN // 2)
         for g in range(2):
-            rows = bank(4 + g, "gate_rows%d" % g, [P, RUN // 2, P])
+            rows = bank(g, "gate_rows%d" % g, [P, RUN // 2, P])
             for b in range(RUN // 2):
                 column = g * RUN // 2 + b
                 nc.tensor.transpose(rows[:, b, :], minus_runs[:, column : column + 1].to_broadcast([P, P]), ident[:])
             nc.scalar.copy(spread[:, g], rows[:].rearrange("p b n -> p n b"))
 
-        x_pairs = sb("x_pairs", [P, PACK * SV], BF16)[:].rearrange("p (u c e) -> p u c e", u=2, e=2)
-        x_planes = sb_at("x_planes", [P, PACK * (S - SV)], BF16, 4 * T * PACK)[:].rearrange("p (j c) -> p j c", j=PACK)
+        def offsets(start, stop):
+            return offs_sb[:, start // LANES : stop // LANES]
+
+        pairs = [
+            sb("pairs%d" % n, [P, PACK * (stop - start)], BF16)[:].rearrange("p (u c e) -> p u c e", u=2, e=2)
+            for n, (start, stop) in enumerate(V_PIECES)
+        ]
+        width_s = S_PIECE[1] - S_PIECE[0]
+        planes = sb_at("planes", [P, PACK * width_s], BF16, 0)[:].rearrange("p (j c) -> p j c", j=PACK)
         for j in range(PACK):
-            nc.vector.tensor_copy(x_pairs[:, j // 2, :, j % 2], x_slots[j][:].indirect(offs_sb[:, : SV // LANES]))
-            nc.scalar.activation(x_planes[:, j, :], x_slots[j][:].indirect(offs_sb[:, SV // LANES :]), COPY)
-        grouped_v = sb("grouped_v", [P, SV, PACK], BF16)
-        grouped_s = sb("grouped_s", [P, S - SV, PACK], BF16)
+            for n, piece in enumerate(V_PIECES):
+                nc.vector.tensor_copy(pairs[n][:, j // 2, :, j % 2], x_slots[j][:].indirect(offsets(*piece)))
+            nc.scalar.activation(planes[:, j, :], x_slots[j][:].indirect(offsets(*S_PIECE)), COPY)
+        dealt = {}
+        CODES, FIRST_TERM, RAW3 = 1024, 2048, 4096
+        PLANE0 = 6144
+        w1_planes = [sb("w1_plane%d" % t, [P, P], U8) if t else sb_at("w1_plane0", [P, P], U8, PLANE0) for t in range(TILES)]
+        w1_codes = {}
 
-        dealt = [sb_at("dealt%d" % t, [P, P, PACK], BF16, 4 * T * (2 if t == 0 else 3) + T * t) for t in range(TILES)]
-        w1_codes = [sb("w1_codes%d" % t, [P, P], U32) for t in range(TILES)]
-        w1_planes = [sb("w1_plane%d" % t, [P, P], U8) for t in range(TILES)]
-
-        def deal(t, engine_copy):
-            engine_copy(
+        def deal(t):
+            at = PLANE0 if t == 3 else X_AT + 4 * T * (3 if t else 2) + T * t
+            dealt[t] = sb_at("dealt%d" % t, [P, P, PACK], BF16, at)
+            nc.scalar.copy(
                 dealt[t][:].rearrange("p (c i) j -> p c j i", i=4), w1_raw[t][:].rearrange("p j (c i) -> p c j i", i=4)
             )
 
         def quantize_w1(t):
+            name = "w1_codes%d" % t
+            w1_codes[t] = sb(name, [P, P], U32) if t == 1 else sb_at(name, [P, P], U32, FIRST_TERM if t == 3 else CODES)
             nc.vector.quantize_mx(w1_codes[t][:].bitcast(FP8X4), w1_planes[t][:], dealt[t][:].rearrange("p c j -> p (c j)"))
 
-        deal(0, nc.scalar.copy)
+        deal(0)
+        grouped = sb("grouped", [P, S_PIECE[0] * PACK], BF16)
+        grouped_s = sb("grouped_s", [P, width_s * PACK], BF16)
+        for n, (start, stop) in enumerate(V_PIECES):
+            nc.vector.tensor_copy(
+                grouped[:, PACK * start : PACK * stop].rearrange("p (c u e) -> p c u e", u=2, e=2),
+                pairs[n].rearrange("p u c e -> p c u e"),
+            )
         nc.scalar.copy(
-            grouped_s[:].rearrange("p (c i) j -> p c j i", i=4), x_planes.rearrange("p j (c i) -> p c j i", i=4)
-        )
-        nc.vector.tensor_copy(
-            grouped_v[:].rearrange("p c (u e) -> p c u e", e=2), x_pairs.rearrange("p u c e -> p c u e")
+            grouped_s[:].rearrange("p (c i j) -> p c j i", i=4, j=PACK), planes.rearrange("p j (c i) -> p c j i", i=4)
         )
         quantize_w1(0)
         x_codes = sb("x_codes", [P, S], U32)
-        x_plane = sb_at("x_plane", [P, S], U8, 4 * T * 2)
-        for start, stop in PIECES:
-            source = grouped_v[:, start:stop, :] if stop <= SV else grouped_s[:]
-            nc.vector.quantize_mx(
-                x_codes[:, start:stop].bitcast(FP8X4), x_plane[:, start:stop], source.rearrange("p c j -> p (c j)")
-            )
+        x_plane = sb_at("x_plane", [P, S], U8, X_AT + 4 * T * 2)
+
+        def quantize_x(start, stop):
+            source = grouped[:, PACK * start : PACK * stop] if stop <= S_PIECE[0] else grouped_s[:]
+            nc.vector.quantize_mx(x_codes[:, start:stop].bitcast(FP8X4), x_plane[:, start:stop], source)
 
         h = [sb("h%d" % t, [P, S], F32) for t in range(TILES)]
+        accs = {}
 
-        def first_product(t, number, start, stop, engine_copy):
-            acc = bank(number, "acc%d_%d" % (t, start), [P, stop - start])
+        def first_product(t, number, start, stop):
+            accs[t, start] = bank(number, "acc%d_%d" % (t, start), [P, stop - start])
             nc.tensor.matmul_mx(
-                acc[:], w1_codes[t][:].bitcast(FP8X4), w1_planes[t][:],
+                accs[t, start][:], w1_codes[t][:].bitcast(FP8X4), w1_planes[t][:],
                 x_codes[:, start:stop].bitcast(FP8X4), x_plane[:, start:stop], start=True, stop=True,
             )
-            engine_copy(h[t][:, start:stop], acc[:])
 
-        deal(1, nc.scalar.copy)
-        deal(2, nc.scalar.copy)
-        for number, (start, stop) in enumerate(PIECES):
-            first_product(0, number, start, stop, nc.scalar.copy if number else nc.vector.tensor_copy)
+        deal(1)
+        deal(2)
+        quantize_x(*PIECES[0])
+        quantize_x(*PIECES[1])
+        quantize_x(*PIECES[2])
         quantize_w1(1)
+        for n, (start, stop) in enumerate(PIECES):
+            first_product(0, 2 + n, start, stop)
+            (nc.scalar.copy if n else nc.vector.tensor_copy)(h[0][:, start:stop], accs[0, start][:])
+        deal(3)
+        first_product(1, 6, 0, S)
         quantize_w1(2)
+        first_product(2, 7, 0, S)
 
         turned = [sb("turned%d" % half, [P, 2, P, 2], BF16) for half in range(2)]
-        sums = [
-            [bank(first + half, "sum%d_%d" % (t, half), [P, P]) for half in range(2)]
-            for t, first in enumerate((4, 6, 2, 0))
-        ]
-
+        early = [bank(half, "early%d" % half, [P, (TILES - 1) * P]) for half in range(2)]
+        late = [bank(3 + half, "late%d" % half, [P, P]) for half in range(2)]
         added = {(t, half): 0 for t in range(TILES) for half in range(2)}
 
         def add_turned(t, term, halves=(0, 1)):
             for half in halves:
                 nc.tensor.matmul(
-                    sums[t][half][:], term[:, half * P : (half + 1) * P], ident[:],
+                    late[half][:] if t == TILES - 1 else early[half][:, t * P : (t + 1) * P], term[:, half * P : (half + 1) * P], ident[:],
                     start=added[t, half] == 0, stop=added[t, half] == D, is_transpose=True,
                 )
                 added[t, half] = added[t, half] + 1
 
-        raws = [sb("raw%d" % t, [P, count, V], F32) if count else None for t, count in enumerate(RAWS)]
+        raws = [sb("raw%d" % t, [P, count, V], F32) if t < 3 else sb_at("raw3", [P, count, V], F32, RAW3) for t, count in enumerate(RAWS)]
         owns = [sb("own%d" % t, [P, V], F32) for t in range(TILES)]
+        terms = {
+            (t, u): sb_at("term0_0", [P, V], F32, FIRST_TERM) if (t, u) == (0, 0) else sb("term%d_%d" % (t, u), [P, V], F32)
+            for t in range(TILES) for u in range(D - RAWS[t]) if (t, u) != (3, 2)
+        }
+        weighed = [sb("weighed%d" % t, [P, count, V], F32) for t, count in enumerate(RAWS)]
 
         def fetch_raw(t):
             for n in range(RAWS[t]):
@@ -171,60 +197,52 @@ def tile_picked_lapl_none_e_kernel(
 
         def fetch_own(t):
             nc.scalar.activation(owns[t][:], h[t][:].indirect(cen_sb[:]), COPY)
-
-        terms = [sb("terms%d" % t, [P, D, V], F32) for t in range(TILES)]
+            add_turned(t, owns[t][:])
 
         def fetch_weighted(t, u):
-            nc.vector.tensor_tensor(terms[t][:, u, :], h[t][:].indirect(pos_sb[u][:]), gates[u], MULT)
-            add_turned(t, terms[t][:, u, :])
+            nc.vector.tensor_tensor(terms[t, u][:], h[t][:].indirect(pos_sb[u][:]), gate_sb[:, u, :], MULT)
+            add_turned(t, terms[t, u][:])
 
-        def weigh(t, halves):
-            cols = slice(halves[0] * P, (halves[-1] + 1) * P)
-            first = D - RAWS[t]
-            nc.vector.tensor_tensor(terms[t][:, first:, cols], raws[t][:, :, cols], gate_sb[:, first:, cols], MULT)
-            for u in range(first, D):
-                add_turned(t, terms[t][:, u, :], halves)
+        def weigh(t):
+            nc.vector.tensor_tensor(weighed[t][:], raws[t][:], gate_sb[:, D - RAWS[t] :, :], MULT)
+            for n in range(RAWS[t]):
+                add_turned(t, weighed[t][:, n, :])
 
-        def cast(t):
-            part = slice(32 * t, 32 * (t + 1))
-            for half in range(2):
-                engine_copy = nc.vector.tensor_copy if t == 2 or (t, half) == (3, 1) else nc.scalar.copy
-                engine_copy(turned[half][:, :, part, :], sums[t][half][:].rearrange("v (q u e) -> v u q e", u=2, e=2))
+        def cast(sums, part, half, engine_copy):
+            engine_copy(turned[half][:, :, part, :], sums[half][:].rearrange("v (q u e) -> v u q e", u=2, e=2))
 
-        def vector_terms(t):
+        for t in range(TILES):
+            last = t + 1 == TILES
+            fetch_raw(t)
+            if not last:
+                nc.scalar.copy(h[t + 1][:], accs[t + 1, 0][:])
             fetch_weighted(t, 0)
             fetch_weighted(t, 1)
-            add_turned(t, owns[t][:])
-            weigh(t, (0, 1))
-            fetch_weighted(t, 2)
-
-        for t in range(TILES - 1):
-            fetch_raw(t)
+            weigh(t)
             fetch_own(t)
-            first_product(t + 1, (3, 0, 1)[t], 0, S, nc.scalar.copy)
-            if t == 0:
-                deal(3, nc.scalar.copy)
-            if t == 1:
-                cast(0)
-            vector_terms(t)
+            if RAWS[t] == 1 and not last:
+                fetch_weighted(t, 2)
             if t == 0:
                 quantize_w1(3)
-        fetch_raw(3)
-        fetch_own(3)
-        cast(1)
-        fetch_weighted(3, 0)
-        fetch_weighted(3, 1)
+                first_product(3, 2, 0, S)
+        terms[3, 2] = sb_at("last_term", [P, V], F32, RAW3)
         for half in range(2):
-            weigh(3, (half,))
-            add_turned(3, owns[3][:], (half,))
-        cast(2)
-        cast(3)
+            cols = slice(half * P, (half + 1) * P)
+            nc.vector.tensor_tensor(
+                terms[3, 2][:, cols], h[3][:].indirect(pos_sb[2][:, half * P // LANES : (half + 1) * P // LANES]),
+                gate_sb[:, 2, cols], MULT,
+            )
+            add_turned(3, terms[3, 2][:], (half,))
+        for half in range(2):
+            cast(early, slice(0, 96), half, nc.scalar.copy)
+        cast(late, slice(96, P), 0, nc.scalar.copy)
+        cast(late, slice(96, P), 1, nc.vector.tensor_copy)
 
         out_rows = out.rearrange("(m p) v -> p m v", p=P)
         copies = (nc.scalar.copy, nc.vector.tensor_copy)
         z_grouped = [sb("z_grouped%d" % half, [P, P, PACK], BF16) for half in range(2)]
         for half in range(2):
-            back = bank(4 + half, "back%d" % half, [P, 2, P])
+            back = bank(5 + half, "back%d" % half, [P, 2, P])
             words = turned[half][:].rearrange("v u p e -> v (u p e)").bitcast(F32)
             for u in range(2):
                 nc.tensor.transpose(back[:, u, :], words[:, u * P : (u + 1) * P], ident[:])
@@ -239,7 +257,7 @@ def tile_picked_lapl_none_e_kernel(
                 z_codes[:].bitcast(FP8X4), z_plane[:], z_grouped[half][:].rearrange("p v j -> p (v j)")
             )
             for m in range(2):
-                acc = bank((6, 7, 2, 3)[2 * half + m], "result%d_%d" % (half, m), [P, P])
+                acc = bank((0, 1, 7, 2)[2 * half + m], "result%d_%d" % (half, m), [P, P])
                 cols = slice(m * P, (m + 1) * P)
                 nc.tensor.matmul_mx(
                     acc[:], w2_codes[:, cols].bitcast(FP8X4), w2_plane[:, cols],

@@ -22,10 +22,11 @@ TILES = H // P
 LANES = 16
 RUN = D * V // P
 RAWS = (1, 1, 2, 1)
-V_PIECES = ((0, 384),)
+V_PIECES = ((0, 256),)
 X_AT = 8192
-S_PIECE = (384, 512)
-PIECES = ((0, 256), (256, 384), (384, 512))
+RAW_AT = X_AT + 4 * T * PACK
+S_PIECE = (256, 512)
+PIECES = ((256, 384), (0, 256), (384, 512))
 
 
 def tile_picked_lapl_none_e_kernel(
@@ -61,7 +62,7 @@ def tile_picked_lapl_none_e_kernel(
         for j in range(1, PACK):
             nc.sync.dma_start(x_slots[j][:], x_rows[j])
         w1_rows = w1.rearrange("(p j) c -> p j c", j=PACK)
-        w1_raw = [sb("w1_raw%d" % t, [P, PACK, P], F32) for t in range(TILES)]
+        w1_raw = [sb_at("w1_raw%d" % t, [P, PACK, P], F32, RAW_AT + 4 * PACK * P * t) for t in range(TILES)]
         cen_sb = sb("cen_sb", [P, V // LANES], U16)
         pos_sb = [sb("pos_sb%d" % u, [P, V // LANES], U16) for u in range(D)]
         gate_sb = sb("gate_sb", [P, D, V], F32)
@@ -110,13 +111,13 @@ def tile_picked_lapl_none_e_kernel(
                 nc.vector.tensor_copy(pairs[n][:, j // 2, :, j % 2], x_slots[j][:].indirect(offsets(*piece)))
             nc.scalar.activation(planes[:, j, :], x_slots[j][:].indirect(offsets(*S_PIECE)), COPY)
         dealt = {}
-        CODES, FIRST_TERM, RAW3 = 1024, 2048, 4096
+        CODES, RAW3 = 2048, 4096
         PLANE0 = 6144
         w1_planes = [sb("w1_plane%d" % t, [P, P], U8) if t else sb_at("w1_plane0", [P, P], U8, PLANE0) for t in range(TILES)]
         w1_codes = {}
 
         def deal(t):
-            at = PLANE0 if t == 3 else X_AT + 4 * T * (3 if t else 2) + T * t
+            at = PLANE0 if t == 3 else X_AT + 4 * T * (3 if t else 2) + T * (t + 1)
             dealt[t] = sb_at("dealt%d" % t, [P, P, PACK], BF16, at)
             nc.scalar.copy(
                 dealt[t][:].rearrange("p (c i) j -> p c j i", i=4), w1_raw[t][:].rearrange("p j (c i) -> p c j i", i=4)
@@ -124,29 +125,34 @@ def tile_picked_lapl_none_e_kernel(
 
         def quantize_w1(t):
             name = "w1_codes%d" % t
-            w1_codes[t] = sb(name, [P, P], U32) if t == 1 else sb_at(name, [P, P], U32, FIRST_TERM if t == 3 else CODES)
+            w1_codes[t] = sb(name, [P, P], U32) if t % 2 else sb_at(name, [P, P], U32, CODES)
             nc.vector.quantize_mx(w1_codes[t][:].bitcast(FP8X4), w1_planes[t][:], dealt[t][:].rearrange("p c j -> p (c j)"))
 
         deal(0)
-        grouped = sb("grouped", [P, S_PIECE[0] * PACK], BF16)
-        grouped_s = sb("grouped_s", [P, width_s * PACK], BF16)
-        for n, (start, stop) in enumerate(V_PIECES):
-            nc.vector.tensor_copy(
-                grouped[:, PACK * start : PACK * stop].rearrange("p (c u e) -> p c u e", u=2, e=2),
-                pairs[n].rearrange("p u c e -> p c u e"),
+        grouped = [
+            sb_at("grouped1", [P, 256 * PACK], BF16, X_AT + 4 * T * 3) if n == 1 else sb("grouped%d" % n, [P, P * PACK], BF16)
+            for n in range(3)
+        ]
+
+        def weave_planes(n, engine_copy):
+            start, stop = PIECES[n]
+            engine_copy(
+                grouped[n][:].rearrange("p (c i j) -> p c j i", i=4, j=PACK),
+                planes[:, :, start - S_PIECE[0] : stop - S_PIECE[0]].rearrange("p j (c i) -> p c j i", i=4),
             )
-        nc.scalar.copy(
-            grouped_s[:].rearrange("p (c i j) -> p c j i", i=4, j=PACK), planes.rearrange("p j (c i) -> p c j i", i=4)
+
+        weave_planes(0, nc.vector.tensor_copy)
+        nc.vector.tensor_copy(
+            grouped[1][:].rearrange("p (c u e) -> p c u e", u=2, e=2), pairs[0].rearrange("p u c e -> p c u e")
         )
-        quantize_w1(0)
+        weave_planes(2, nc.scalar.copy)
         x_codes = sb("x_codes", [P, S], U32)
-        x_plane = sb_at("x_plane", [P, S], U8, X_AT + 4 * T * 2)
+        x_plane = sb("x_plane", [P, S], U8)
 
-        def quantize_x(start, stop):
-            source = grouped[:, PACK * start : PACK * stop] if stop <= S_PIECE[0] else grouped_s[:]
-            nc.vector.quantize_mx(x_codes[:, start:stop].bitcast(FP8X4), x_plane[:, start:stop], source)
+        def quantize_x(n):
+            start, stop = PIECES[n]
+            nc.vector.quantize_mx(x_codes[:, start:stop].bitcast(FP8X4), x_plane[:, start:stop], grouped[n][:])
 
-        h = [sb("h%d" % t, [P, S], F32) for t in range(TILES)]
         accs = {}
 
         def first_product(t, number, start, stop):
@@ -158,19 +164,20 @@ def tile_picked_lapl_none_e_kernel(
 
         deal(1)
         deal(2)
-        quantize_x(*PIECES[0])
-        quantize_x(*PIECES[1])
-        quantize_x(*PIECES[2])
+        h = [sb("h%d" % t, [P, S], F32) if t else sb_at("h0", [P, S], F32, RAW_AT + 4 * PACK * P) for t in range(TILES)]
+        quantize_x(0)
+        quantize_x(1)
+        quantize_w1(0)
+        quantize_x(2)
         quantize_w1(1)
         for n, (start, stop) in enumerate(PIECES):
             first_product(0, 2 + n, start, stop)
-            (nc.scalar.copy if n else nc.vector.tensor_copy)(h[0][:, start:stop], accs[0, start][:])
+            (nc.scalar.copy if n == 2 else nc.vector.tensor_copy)(h[0][:, start:stop], accs[0, start][:])
         deal(3)
         first_product(1, 6, 0, S)
         quantize_w1(2)
         first_product(2, 7, 0, S)
 
-        turned = [sb("turned%d" % half, [P, 2, P, 2], BF16) for half in range(2)]
         early = [bank(half, "early%d" % half, [P, (TILES - 1) * P]) for half in range(2)]
         late = [bank(3 + half, "late%d" % half, [P, P]) for half in range(2)]
         added = {(t, half): 0 for t in range(TILES) for half in range(2)}
@@ -183,10 +190,10 @@ def tile_picked_lapl_none_e_kernel(
                 )
                 added[t, half] = added[t, half] + 1
 
-        raws = [sb("raw%d" % t, [P, count, V], F32) if t < 3 else sb_at("raw3", [P, count, V], F32, RAW3) for t, count in enumerate(RAWS)]
-        owns = [sb("own%d" % t, [P, V], F32) for t in range(TILES)]
+        raws = [sb("raw%d" % t, [P, count, V], F32) if t < 3 else sb_at("raw3", [P, count, V], F32, 7168) for t, count in enumerate(RAWS)]
+        owns = [sb_at("own2", [P, V], F32, RAW3) if t == 2 else sb("own%d" % t, [P, V], F32) for t in range(TILES)]
         terms = {
-            (t, u): sb_at("term0_0", [P, V], F32, FIRST_TERM) if (t, u) == (0, 0) else sb("term%d_%d" % (t, u), [P, V], F32)
+            (t, u): sb_at("term0_2", [P, V], F32, RAW_AT + 4 * PACK * P * 3) if (t, u) == (0, 2) else sb("term%d_%d" % (t, u), [P, V], F32)
             for t in range(TILES) for u in range(D - RAWS[t]) if (t, u) != (3, 2)
         }
         weighed = [sb("weighed%d" % t, [P, count, V], F32) for t, count in enumerate(RAWS)]
@@ -217,14 +224,14 @@ def tile_picked_lapl_none_e_kernel(
             if not last:
                 nc.scalar.copy(h[t + 1][:], accs[t + 1, 0][:])
             fetch_weighted(t, 0)
+            if t == 0:
+                quantize_w1(3)
+                first_product(3, 2, 0, S)
             fetch_weighted(t, 1)
             weigh(t)
             fetch_own(t)
             if RAWS[t] == 1 and not last:
                 fetch_weighted(t, 2)
-            if t == 0:
-                quantize_w1(3)
-                first_product(3, 2, 0, S)
         terms[3, 2] = sb_at("last_term", [P, V], F32, RAW3)
         for half in range(2):
             cols = slice(half * P, (half + 1) * P)
@@ -233,8 +240,9 @@ def tile_picked_lapl_none_e_kernel(
                 gate_sb[:, 2, cols], MULT,
             )
             add_turned(3, terms[3, 2][:], (half,))
-        for half in range(2):
-            cast(early, slice(0, 96), half, nc.scalar.copy)
+        turned = [sb("turned0", [P, 2, P, 2], BF16), sb_at("turned1", [P, 2, P, 2], BF16, 7168)]
+        cast(early, slice(0, 96), 0, nc.scalar.copy)
+        cast(early, slice(0, 96), 1, nc.vector.tensor_copy)
         cast(late, slice(96, P), 0, nc.scalar.copy)
         cast(late, slice(96, P), 1, nc.vector.tensor_copy)
 

@@ -15,14 +15,16 @@ U8 = mybir.dt.uint8
 FP8X4 = mybir.dt.float8_e4m3fn_x4
 COPY = mybir.ActivationFunctionType.Copy
 MULT = mybir.AluOpType.mult
+SUB = mybir.AluOpType.subtract
 
 P = 128
 PACK = 4
 TILES = H // P
 LANES = 16
 RUN = D * V // P
-RAWS = (1, 1, 2, 1)
+RAWS = (1, 1, 1, 1)
 V_PIECES = ((0, 256),)
+BARE = 3
 X_AT = 8192
 RAW_AT = X_AT + 4 * T * PACK
 S_PIECE = (256, 512)
@@ -80,6 +82,11 @@ def tile_picked_lapl_none_e_kernel(
         nc.sync.dma_start(pos_sb[2][:], pos[2])
         load_w1(3)
         nc.sync.dma_start(cen_sb[:], cen)
+        gate_cols = sb("gate_cols", [P, 2], F32)
+        first = (D - 1) * P * V - P
+        diagonal = gate.rearrange("d p v -> (d p v)")[first:].rearrange("(p x) -> p x", x=V + 1)[:, P::P]
+        with nc.allow_non_contiguous_dma(reason="one value a partition and half"):
+            nc.sync.dma_start(gate_cols[:], diagonal)
         w2_codes = sb("w2_codes", [P, N], U32)
         nc.sync.dma_start(w2_codes[:].bitcast(I32), w2_words[0].rearrange("p n t -> p (n t)").bitcast(I32))
         for r in range(4):
@@ -172,7 +179,7 @@ def tile_picked_lapl_none_e_kernel(
         quantize_w1(1)
         for n, (start, stop) in enumerate(PIECES):
             first_product(0, 2 + n, start, stop)
-            (nc.scalar.copy if n == 2 else nc.vector.tensor_copy)(h[0][:, start:stop], accs[0, start][:])
+            (nc.scalar.copy if n != 1 else nc.vector.tensor_copy)(h[0][:, start:stop], accs[0, start][:])
         deal(3)
         first_product(1, 6, 0, S)
         quantize_w1(2)
@@ -180,13 +187,14 @@ def tile_picked_lapl_none_e_kernel(
 
         early = [bank(half, "early%d" % half, [P, (TILES - 1) * P]) for half in range(2)]
         late = [bank(3 + half, "late%d" % half, [P, P]) for half in range(2)]
+        bare = [bank(5 + half, "bare%d" % half, [P, BARE * P]) for half in range(2)]
         added = {(t, half): 0 for t in range(TILES) for half in range(2)}
 
         def add_turned(t, term, halves=(0, 1)):
             for half in halves:
                 nc.tensor.matmul(
                     late[half][:] if t == TILES - 1 else early[half][:, t * P : (t + 1) * P], term[:, half * P : (half + 1) * P], ident[:],
-                    start=added[t, half] == 0, stop=added[t, half] == D, is_transpose=True,
+                    start=added[t, half] == 0, stop=added[t, half] == (D - 1 if t < BARE else D), is_transpose=True,
                 )
                 added[t, half] = added[t, half] + 1
 
@@ -196,7 +204,7 @@ def tile_picked_lapl_none_e_kernel(
             (t, u): sb_at("term0_2", [P, V], F32, RAW_AT + 4 * PACK * P * 3) if (t, u) == (0, 2) else sb("term%d_%d" % (t, u), [P, V], F32)
             for t in range(TILES) for u in range(D - RAWS[t]) if (t, u) != (3, 2)
         }
-        weighed = [sb("weighed%d" % t, [P, count, V], F32) for t, count in enumerate(RAWS)]
+        weighed = {t: sb("weighed%d" % t, [P, RAWS[t], V], F32) for t in range(BARE, TILES)}
 
         def fetch_raw(t):
             for n in range(RAWS[t]):
@@ -211,12 +219,16 @@ def tile_picked_lapl_none_e_kernel(
             add_turned(t, terms[t, u][:])
 
         def weigh(t):
+            if t < BARE:
+                for half in range(2):
+                    nc.tensor.transpose(bare[half][:, t * P : (t + 1) * P], raws[t][:, 0, half * P : (half + 1) * P], ident[:])
+                return
             nc.vector.tensor_tensor(weighed[t][:], raws[t][:], gate_sb[:, D - RAWS[t] :, :], MULT)
             for n in range(RAWS[t]):
                 add_turned(t, weighed[t][:, n, :])
 
-        def cast(sums, part, half, engine_copy):
-            engine_copy(turned[half][:, :, part, :], sums[half][:].rearrange("v (q u e) -> v u q e", u=2, e=2))
+        def paired(rows):
+            return rows.rearrange("v (q u e) -> v u q e", u=2, e=2)
 
         for t in range(TILES):
             last = t + 1 == TILES
@@ -240,17 +252,22 @@ def tile_picked_lapl_none_e_kernel(
                 gate_sb[:, 2, cols], MULT,
             )
             add_turned(3, terms[3, 2][:], (half,))
-        turned = [sb("turned0", [P, 2, P, 2], BF16), sb_at("turned1", [P, 2, P, 2], BF16, 7168)]
-        cast(early, slice(0, 96), 0, nc.scalar.copy)
-        cast(early, slice(0, 96), 1, nc.vector.tensor_copy)
-        cast(late, slice(96, P), 0, nc.scalar.copy)
-        cast(late, slice(96, P), 1, nc.vector.tensor_copy)
+        turned = [sb_at("turned%d" % half, [P, 2, P, 2], BF16, 7168 - 512 + 1024 * half) for half in range(2)]
+        scaled = [sb("scaled%d" % half, [P, BARE * P], F32) for half in range(2)]
+        for half in range(2):
+            nc.scalar.activation(scaled[half][:], bare[half][:], COPY, scale=gate_cols[:, half : half + 1])
+        for half in range(2):
+            nc.vector.tensor_tensor(
+                turned[half][:, :, : 32 * BARE, :], paired(early[half][:, : BARE * P]), paired(scaled[half][:]), SUB
+            )
+        nc.scalar.copy(turned[0][:, :, 96:, :], paired(late[0][:]))
+        nc.scalar.copy(turned[1][:, :, 96:, :], paired(late[1][:]))
 
         out_rows = out.rearrange("(m p) v -> p m v", p=P)
         copies = (nc.scalar.copy, nc.vector.tensor_copy)
         z_grouped = [sb("z_grouped%d" % half, [P, P, PACK], BF16) for half in range(2)]
         for half in range(2):
-            back = bank(5 + half, "back%d" % half, [P, 2, P])
+            back = bank((7, 2)[half], "back%d" % half, [P, 2, P])
             words = turned[half][:].rearrange("v u p e -> v (u p e)").bitcast(F32)
             for u in range(2):
                 nc.tensor.transpose(back[:, u, :], words[:, u * P : (u + 1) * P], ident[:])
@@ -265,7 +282,7 @@ def tile_picked_lapl_none_e_kernel(
                 z_codes[:].bitcast(FP8X4), z_plane[:], z_grouped[half][:].rearrange("p v j -> p (v j)")
             )
             for m in range(2):
-                acc = bank((0, 1, 7, 2)[2 * half + m], "result%d_%d" % (half, m), [P, P])
+                acc = bank((5, 6, 3, 4)[2 * half + m], "result%d_%d" % (half, m), [P, P])
                 cols = slice(m * P, (m + 1) * P)
                 nc.tensor.matmul_mx(
                     acc[:], w2_codes[:, cols].bitcast(FP8X4), w2_plane[:, cols],

@@ -23,7 +23,6 @@ TILES = H // P
 LANES = 16
 RUN = D * V // P
 RAWS = (1, 1, 1, 1)
-V_PIECES = ((0, 256),)
 BARE = 3
 X_AT = 8192
 RAW_AT = X_AT + 4 * T * PACK
@@ -73,13 +72,10 @@ def tile_picked_lapl_none_e_kernel(
         def load_w1(t):
             nc.sync.dma_start(w1_raw[t][:], w1_rows[:, :, t * P : (t + 1) * P])
 
-        load_w1(0)
-        nc.sync.dma_start(pos_sb[3][:], pos[3])
-        load_w1(1)
-        nc.sync.dma_start(pos_sb[0][:], pos[0])
-        nc.sync.dma_start(pos_sb[1][:], pos[1])
-        load_w1(2)
-        nc.sync.dma_start(pos_sb[2][:], pos[2])
+        for t in range(3):
+            load_w1(t)
+        for u in (0, 3, 1, 2):
+            nc.sync.dma_start(pos_sb[u][:], pos[u])
         load_w1(3)
         nc.sync.dma_start(cen_sb[:], cen)
         gate_cols = sb("gate_cols", [P, 2], F32)
@@ -107,15 +103,11 @@ def tile_picked_lapl_none_e_kernel(
         def offsets(start, stop):
             return offs_sb[:, start // LANES : stop // LANES]
 
-        pairs = [
-            sb("pairs%d" % n, [P, PACK * (stop - start)], BF16)[:].rearrange("p (u c e) -> p u c e", u=2, e=2)
-            for n, (start, stop) in enumerate(V_PIECES)
-        ]
+        grouped = [sb("grouped%d" % n, [P, (stop - start) * PACK], BF16) for n, (start, stop) in enumerate(PIECES)]
         width_s = S_PIECE[1] - S_PIECE[0]
         planes = sb_at("planes", [P, PACK * width_s], BF16, 0)[:].rearrange("p (j c) -> p j c", j=PACK)
         for j in range(PACK):
-            for n, piece in enumerate(V_PIECES):
-                nc.vector.tensor_copy(pairs[n][:, j // 2, :, j % 2], x_slots[j][:].indirect(offsets(*piece)))
+            nc.vector.tensor_copy(grouped[1][:, j::PACK], x_slots[j][:].indirect(offsets(*PIECES[1])))
             nc.scalar.activation(planes[:, j, :], x_slots[j][:].indirect(offsets(*S_PIECE)), COPY)
         dealt = {}
         CODES, RAW3 = 2048, 4096
@@ -136,10 +128,6 @@ def tile_picked_lapl_none_e_kernel(
             nc.vector.quantize_mx(w1_codes[t][:].bitcast(FP8X4), w1_planes[t][:], dealt[t][:].rearrange("p c j -> p (c j)"))
 
         deal(0)
-        grouped = [
-            sb_at("grouped1", [P, 256 * PACK], BF16, X_AT + 4 * T * 3) if n == 1 else sb("grouped%d" % n, [P, P * PACK], BF16)
-            for n in range(3)
-        ]
 
         def weave_planes(n, engine_copy):
             start, stop = PIECES[n]
@@ -149,11 +137,8 @@ def tile_picked_lapl_none_e_kernel(
             )
 
         weave_planes(0, nc.vector.tensor_copy)
-        nc.vector.tensor_copy(
-            grouped[1][:].rearrange("p (c u e) -> p c u e", u=2, e=2), pairs[0].rearrange("p u c e -> p c u e")
-        )
         weave_planes(2, nc.scalar.copy)
-        x_codes = sb("x_codes", [P, S], U32)
+        x_codes = sb_at("x_codes", [P, S], U32, X_AT + 4 * T * 3)
         x_plane = sb("x_plane", [P, S], U8)
 
         def quantize_x(n):
@@ -163,23 +148,28 @@ def tile_picked_lapl_none_e_kernel(
         accs = {}
 
         def first_product(t, number, start, stop):
-            accs[t, start] = bank(number, "acc%d_%d" % (t, start), [P, stop - start])
+            if (t, start) not in accs:
+                accs[t, start] = bank(number, "acc%d_%d" % (t, start), [P, stop - start])
             nc.tensor.matmul_mx(
-                accs[t, start][:], w1_codes[t][:].bitcast(FP8X4), w1_planes[t][:],
+                accs[t, start][:, : stop - start], w1_codes[t][:].bitcast(FP8X4), w1_planes[t][:],
                 x_codes[:, start:stop].bitcast(FP8X4), x_plane[:, start:stop], start=True, stop=True,
             )
 
         deal(1)
         deal(2)
-        h = [sb("h%d" % t, [P, S], F32) if t else sb_at("h0", [P, S], F32, RAW_AT + 4 * PACK * P) for t in range(TILES)]
-        quantize_x(0)
+        h = [sb("h%d" % t, [P, S], F32) for t in range(TILES)]
         quantize_x(1)
         quantize_w1(0)
+        quantize_x(0)
         quantize_x(2)
         quantize_w1(1)
-        for n, (start, stop) in enumerate(PIECES):
+        small = bank(2, "small", [P, 256])
+        accs[0, 256], accs[0, 384] = small[:, :P], small[:, P:]
+        for n in (1, 0, 2):
+            start, stop = PIECES[n]
             first_product(0, 2 + n, start, stop)
-            (nc.scalar.copy if n != 1 else nc.vector.tensor_copy)(h[0][:, start:stop], accs[0, start][:])
+        nc.vector.tensor_copy(h[0][:, :256], accs[0, 0][:])
+        nc.scalar.copy(h[0][:, 256:], small[:])
         deal(3)
         first_product(1, 6, 0, S)
         quantize_w1(2)

from contextlib import ExitStack

import concourse.mybir as mybir
from concourse.masks import make_identity

K, T, S, D, V, H, N = 512, 1024, 512, 4, 256, 512, 256
FLOPS = 2 * K * H * S + 2 * H * N * V

F32 = mybir.dt.float32
BF16 = mybir.dt.bfloat16
I32 = mybir.dt.int32
U32 = mybir.dt.uint32
U16 = mybir.dt.uint16
U8 = mybir.dt.uint8
FP8X4 = mybir.dt.float8_e4m3fn_x4
COPY = mybir.ActivationFunctionType.Copy
MULT = mybir.AluOpType.mult
SUB = mybir.AluOpType.subtract

P = 128
PACK = 4
TILES = H // P
LANES = 16
RUN = D * V // P
RAWS = (1, 1, 1, 1)
BARE = 3
X_AT = 8192
RAW_AT = X_AT + 4 * T * PACK
S_PIECE = (256, 512)
PIECES = ((256, 384), (0, 256), (384, 512))


def tile_picked_lapl_none_e_kernel(
    tc, xT, w1, w2_words, w2_scales, gate, offs, cen, pos1, pos2, pos3, pos4, out
):
    nc = tc.nc
    with ExitStack() as ctx:
        keep = ctx.enter_context(tc.tile_pool(name="keep", bufs=1))
        placed = ctx.enter_context(tc.tile_pool(name="placed", bufs=1))
        psum = ctx.enter_context(tc.psum_pool(name="psum", bufs=1))

        def sb(name, shape, dtype):
            return keep.tile(shape, dtype, name=name, align_bytes=256)

        def sb_at(name, shape, dtype, offset):
            return placed.tile(shape, dtype, name=name, offset=offset, align_bytes=256)

        def bank(number, name, shape):
            return psum.tile(shape, F32, name=name, tag="bank%d" % number)

        ident = sb("ident", [P, P], F32)
        make_identity(nc, ident[:])
        w2_plane = sb("w2_plane", [P, N], U8)
        nc.gpsimd.memset(w2_plane[:], 0)

        x_rows = xT.rearrange("(p j) t -> j p t", j=PACK)
        x_slots = [sb_at("x_slot%d" % j, [P, T], F32, X_AT + 4 * T * j) for j in range(PACK)]
        offs_sb = sb("offs_sb", [P, S // LANES], U16)
        gate_runs = sb("gate_runs", [P, RUN], F32)
        nc.sync.dma_start(gate_runs[:], gate.rearrange("d p (a b) -> (d p a) b", b=RUN)[:: P + 1, :])
        nc.sync.dma_start(x_slots[0][:], x_rows[0])
        nc.sync.dma_start(offs_sb[:], offs)
        for j in range(1, PACK):
            nc.sync.dma_start(x_slots[j][:], x_rows[j])
        w1_rows = w1.rearrange("(p j) c -> p j c", j=PACK)
        w1_raw = [sb_at("w1_raw%d" % t, [P, PACK, P], F32, RAW_AT + 4 * PACK * P * t) for t in range(TILES)]
        cen_sb = sb("cen_sb", [P, V // LANES], U16)
        pos_sb = [sb("pos_sb%d" % u, [P, V // LANES], U16) for u in range(D)]
        gate_sb = sb("gate_sb", [P, D, V], F32)
        pos = (pos1, pos2, pos3, pos4)

        def load_w1(t):
            nc.sync.dma_start(w1_raw[t][:], w1_rows[:, :, t * P : (t + 1) * P])

        for t in range(3):
            load_w1(t)
        for u in (0, 3, 1, 2):
            nc.sync.dma_start(pos_sb[u][:], pos[u])
        load_w1(3)
        nc.sync.dma_start(cen_sb[:], cen)
        gate_cols = sb("gate_cols", [P, 2], F32)
        first = (D - 1) * P * V - P
        diagonal = gate.rearrange("d p v -> (d p v)")[first:].rearrange("(p x) -> p x", x=V + 1)[:, P::P]
        with nc.allow_non_contiguous_dma(reason="one value a partition and half"):
            nc.sync.dma_start(gate_cols[:], diagonal)
        w2_codes = sb("w2_codes", [P, N], U32)
        nc.sync.dma_start(w2_codes[:].bitcast(I32), w2_words[0].rearrange("p n t -> p (n t)").bitcast(I32))
        for r in range(4):
            nc.sync.dma_start(
                w2_plane[32 * r : 32 * r + 4, :].bitcast(I32), w2_scales[0, 4 * r : 4 * r + 4, :].bitcast(I32)
            )

        minus_runs = sb_at("minus_runs", [P, RUN], F32, 0)
        nc.scalar.activation(minus_runs[:], gate_runs[:], COPY, scale=-1.0)
        spread = gate_sb[:].rearrange("p d (q g b) -> p g (d q) b", g=2, b=RUN // 2)
        for g in range(2):
            rows = bank(g, "gate_rows%d" % g, [P, RUN // 2, P])
            for b in range(RUN // 2):
                column = g * RUN // 2 + b
                nc.tensor.transpose(rows[:, b, :], minus_runs[:, column : column + 1].to_broadcast([P, P]), ident[:])
            nc.scalar.copy(spread[:, g], rows[:].rearrange("p b n -> p n b"))

        def offsets(start, stop):
            return offs_sb[:, start // LANES : stop // LANES]

        grouped = [sb("grouped%d" % n, [P, (stop - start) * PACK], BF16) for n, (start, stop) in enumerate(PIECES)]
        width_s = S_PIECE[1] - S_PIECE[0]
        planes = sb_at("planes", [P, PACK * width_s], BF16, 0)[:].rearrange("p (j c) -> p j c", j=PACK)
        for j in range(PACK):
            nc.vector.tensor_copy(grouped[1][:, j::PACK], x_slots[j][:].indirect(offsets(*PIECES[1])))
            nc.scalar.activation(planes[:, j, :], x_slots[j][:].indirect(offsets(*S_PIECE)), COPY)
        dealt = {}
        CODES, RAW3 = 2048, 4096
        PLANE0 = 6144
        w1_planes = [sb("w1_plane%d" % t, [P, P], U8) if t else sb_at("w1_plane0", [P, P], U8, PLANE0) for t in range(TILES)]
        w1_codes = {}

        def deal(t):
            at = PLANE0 if t == 3 else X_AT + 4 * T * (3 if t else 2) + T * (t + 1)
            dealt[t] = sb_at("dealt%d" % t, [P, P, PACK], BF16, at)
            nc.scalar.copy(
                dealt[t][:].rearrange("p (c i) j -> p c j i", i=4), w1_raw[t][:].rearrange("p j (c i) -> p c j i", i=4)
            )

        def quantize_w1(t):
            name = "w1_codes%d" % t
            w1_codes[t] = sb(name, [P, P], U32) if t % 2 else sb_at(name, [P, P], U32, CODES)
            nc.vector.quantize_mx(w1_codes[t][:].bitcast(FP8X4), w1_planes[t][:], dealt[t][:].rearrange("p c j -> p (c j)"))

        deal(0)

        def weave_planes(n, engine_copy):
            start, stop = PIECES[n]
            engine_copy(
                grouped[n][:].rearrange("p (c i j) -> p c j i", i=4, j=PACK),
                planes[:, :, start - S_PIECE[0] : stop - S_PIECE[0]].rearrange("p j (c i) -> p c j i", i=4),
            )

        weave_planes(0, nc.vector.tensor_copy)
        weave_planes(2, nc.scalar.copy)
        x_codes = sb_at("x_codes", [P, S], U32, X_AT + 4 * T * 3)
        x_plane = sb("x_plane", [P, S], U8)

        def quantize_x(n):
            start, stop = PIECES[n]
            nc.vector.quantize_mx(x_codes[:, start:stop].bitcast(FP8X4), x_plane[:, start:stop], grouped[n][:])

        accs = {}

        def first_product(t, number, start, stop):
            if (t, start) not in accs:
                accs[t, start] = bank(number, "acc%d_%d" % (t, start), [P, stop - start])
            nc.tensor.matmul_mx(
                accs[t, start][:, : stop - start], w1_codes[t][:].bitcast(FP8X4), w1_planes[t][:],
                x_codes[:, start:stop].bitcast(FP8X4), x_plane[:, start:stop], start=True, stop=True,
            )

        deal(1)
        deal(2)
        h = [sb("h%d" % t, [P, S], F32) for t in range(TILES)]
        quantize_x(1)
        quantize_w1(0)
        quantize_x(0)
        quantize_x(2)
        quantize_w1(1)
        small = bank(2, "small", [P, 256])
        accs[0, 256], accs[0, 384] = small[:, :P], small[:, P:]
        for n in (1, 0, 2):
            start, stop = PIECES[n]
            first_product(0, 2 + n, start, stop)
        nc.vector.tensor_copy(h[0][:, :256], accs[0, 0][:])
        nc.scalar.copy(h[0][:, 256:], small[:])
        deal(3)
        first_product(1, 6, 0, S)
        quantize_w1(2)
        first_product(2, 7, 0, S)

        early = [bank(half, "early%d" % half, [P, (TILES - 1) * P]) for half in range(2)]
        late = [bank(3 + half, "late%d" % half, [P, P]) for half in range(2)]
        bare = [bank(5 + half, "bare%d" % half, [P, BARE * P]) for half in range(2)]
        added = {(t, half): 0 for t in range(TILES) for half in range(2)}

        def add_turned(t, term, halves=(0, 1)):
            for half in halves:
                nc.tensor.matmul(
                    late[half][:] if t == TILES - 1 else early[half][:, t * P : (t + 1) * P], term[:, half * P : (half + 1) * P], ident[:],
                    start=added[t, half] == 0, stop=added[t, half] == (D - 1 if t < BARE else D), is_transpose=True,
                )
                added[t, half] = added[t, half] + 1

        raws = [sb("raw%d" % t, [P, count, V], F32) if t < 3 else sb_at("raw3", [P, count, V], F32, 7168) for t, count in enumerate(RAWS)]
        owns = [sb_at("own2", [P, V], F32, RAW3) if t == 2 else sb("own%d" % t, [P, V], F32) for t in range(TILES)]
        terms = {
            (t, u): sb_at("term0_2", [P, V], F32, RAW_AT + 4 * PACK * P * 3) if (t, u) == (0, 2) else sb("term%d_%d" % (t, u), [P, V], F32)
            for t in range(TILES) for u in range(D - RAWS[t]) if (t, u) != (3, 2)
        }
        weighed = {t: sb("weighed%d" % t, [P, RAWS[t], V], F32) for t in range(BARE, TILES)}

        def fetch_raw(t):
            for n in range(RAWS[t]):
                nc.scalar.activation(raws[t][:, n, :], h[t][:].indirect(pos_sb[D - RAWS[t] + n][:]), COPY)

        def fetch_own(t):
            nc.scalar.activation(owns[t][:], h[t][:].indirect(cen_sb[:]), COPY)
            add_turned(t, owns[t][:])

        def fetch_weighted(t, u):
            nc.vector.tensor_tensor(terms[t, u][:], h[t][:].indirect(pos_sb[u][:]), gate_sb[:, u, :], MULT)
            add_turned(t, terms[t, u][:])

        def weigh(t):
            if t < BARE:
                for half in range(2):
                    nc.tensor.transpose(bare[half][:, t * P : (t + 1) * P], raws[t][:, 0, half * P : (half + 1) * P], ident[:])
                return
            nc.vector.tensor_tensor(weighed[t][:], raws[t][:], gate_sb[:, D - RAWS[t] :, :], MULT)
            for n in range(RAWS[t]):
                add_turned(t, weighed[t][:, n, :])

        def paired(rows):
            return rows.rearrange("v (q u e) -> v u q e", u=2, e=2)

        for t in range(TILES):
            last = t + 1 == TILES
            fetch_raw(t)
            if not last:
                nc.scalar.copy(h[t + 1][:], accs[t + 1, 0][:])
            fetch_weighted(t, 0)
            if t == 0:
                quantize_w1(3)
                first_product(3, 2, 0, S)
            fetch_weighted(t, 1)
            weigh(t)
            fetch_own(t)
            if RAWS[t] == 1 and not last:
                fetch_weighted(t, 2)
        terms[3, 2] = sb_at("last_term", [P, V], F32, RAW3)
        for half in range(2):
            cols = slice(half * P, (half + 1) * P)
            nc.vector.tensor_tensor(
                terms[3, 2][:, cols], h[3][:].indirect(pos_sb[2][:, half * P // LANES : (half + 1) * P // LANES]),
                gate_sb[:, 2, cols], MULT,
            )
            add_turned(3, terms[3, 2][:], (half,))
        turned = [sb_at("turned%d" % half, [P, 2, P, 2], BF16, 7168 - 512 + 1024 * half) for half in range(2)]
        scaled = [sb("scaled%d" % half, [P, BARE * P], F32) for half in range(2)]
        for half in range(2):
            nc.scalar.activation(scaled[half][:], bare[half][:], COPY, scale=gate_cols[:, half : half + 1])
        for half in range(2):
            nc.vector.tensor_tensor(
                turned[half][:, :, : 32 * BARE, :], paired(early[half][:, : BARE * P]), paired(scaled[half][:]), SUB
            )
        nc.scalar.copy(turned[0][:, :, 96:, :], paired(late[0][:]))
        nc.scalar.copy(turned[1][:, :, 96:, :], paired(late[1][:]))

        out_rows = out.rearrange("(m p) v -> p m v", p=P)
        copies = (nc.scalar.copy, nc.vector.tensor_copy)
        z_grouped = [sb("z_grouped%d" % half, [P, P, PACK], BF16) for half in range(2)]
        for half in range(2):
            back = bank((7, 2)[half], "back%d" % half, [P, 2, P])
            words = turned[half][:].rearrange("v u p e -> v (u p e)").bitcast(F32)
            for u in range(2):
                nc.tensor.transpose(back[:, u, :], words[:, u * P : (u + 1) * P], ident[:])
            nc.scalar.copy(
                z_grouped[half][:].rearrange("p v j -> p (v j)").bitcast(F32).rearrange("p (v u) -> p v u", u=2),
                back[:].rearrange("p u v -> p v u"),
            )
        for half in range(2):
            z_codes = sb("z_codes%d" % half, [P, P], U32)
            z_plane = sb("z_plane%d" % half, [P, P], U8)
            nc.vector.quantize_mx(
                z_codes[:].bitcast(FP8X4), z_plane[:], z_grouped[half][:].rearrange("p v j -> p (v j)")
            )
            for m in range(2):
                acc = bank((5, 6, 3, 4)[2 * half + m], "result%d_%d" % (half, m), [P, P])
                cols = slice(m * P, (m + 1) * P)
                nc.tensor.matmul_mx(
                    acc[:], w2_codes[:, cols].bitcast(FP8X4), w2_plane[:, cols],
                    z_codes[:].bitcast(FP8X4), z_plane[:], start=True, stop=True,
                )
                result = sb("result_sb%d_%d" % (half, m), [P, P], F32)
                copies[m](result[:], acc[:])
                queue = nc.scalar if (half, m) == (1, 0) else nc.sync
                queue.dma_start(out_rows[:, m, half * P : (half + 1) * P], result[:])
